import numpy as np
import ml_dtypes


def mxq(x, axis, fmt="e4m3"):
    dtype, down = {"e4m3": (ml_dtypes.float8_e4m3fn, 7), "e5m2": (ml_dtypes.float8_e5m2, 14)}[fmt]
    v = np.moveaxis(np.asarray(x, np.float32).astype(ml_dtypes.bfloat16).astype(np.float64), axis, -1)
    blocks = v.reshape(v.shape[:-1] + (-1, 32))
    amax = np.abs(blocks).max(-1, keepdims=True)
    byte = np.maximum(np.where(amax > 0, np.frexp(amax)[1] - 1 + 127, 0) - down, 1)
    scale = np.exp2(byte - 127.0)
    codes = (blocks / scale).astype(np.float32).astype(dtype).astype(np.float64)
    return np.moveaxis((codes * scale).reshape(v.shape), -1, axis)


WIDE = False


def mx_kscale(k):
    if not WIDE:
        return np.ones(k)
    levels = np.array([10, -10, 5, -5, 0])
    if k % 512:
        return np.exp2(np.random.permutation(np.resize(levels, k // 32))).repeat(32)
    a = np.empty((k // 512, 16))
    for p in range(k // 512):
        a[p, :8] = np.random.permutation(np.resize(levels, 8))
        for g in range(8):
            far = levels[np.abs(levels - a[p, g]) >= 10]
            a[p, g + 8] = far[np.random.randint(len(far))]
    return np.exp2(a.ravel()).repeat(32)


def f64(x):
    return np.asarray(x).astype(np.float64)


def striped(idx):
    return np.tile(idx.reshape(-1, 16).T, (8, 1)).astype(np.uint16)


def unstriped(offs):
    return offs[:16].T.reshape(-1).astype(np.int64)


E2M1 = np.array([0.0, 0.5, 1.0, 1.5, 2.0, 3.0, 4.0, 6.0, -0.0, -0.5, -1.0, -1.5, -2.0, -3.0, -4.0, -6.0])


def pack_weight(w, fmt):
    k, n = w.shape
    w = f64(np.asarray(w, np.float32).astype(ml_dtypes.bfloat16)).reshape(k // 32, 32, n)
    amax = np.abs(w).max(1)
    if fmt == "e4m3":
        byte = np.frexp(amax)[1] - 1 + 127 - 7
    else:
        mant, ex = np.frexp(amax / 6.0)
        byte = np.where(mant > 0.5, ex, ex - 1) + 127
    byte = np.clip(np.where(amax > 0, byte, 1), 1, 254)
    scaled = (w * np.exp2(127.0 - byte)[:, None, :]).reshape(k, n).astype(np.float32)
    by_word = np.ascontiguousarray(scaled.reshape(k // 512, 128, 4, n).transpose(0, 1, 3, 2))
    if fmt == "e4m3":
        words = by_word.astype(ml_dtypes.float8_e4m3fn).view(np.uint8)
    else:
        c = by_word.astype(ml_dtypes.float4_e2m1fn).view(np.uint8) & 0xF
        words = (c[..., 0::2] | (c[..., 1::2] << 4)).reshape(k // 512, 128, 2 * n)
    return np.ascontiguousarray(words), np.ascontiguousarray(byte.astype(np.uint8).reshape(k // 512, 16, n))


def unpack_weight(words, scales, fmt):
    g, _, n = scales.shape
    words = np.ascontiguousarray(words).reshape(g, 128, n, -1)
    if fmt == "e4m3":
        vals = words.view(ml_dtypes.float8_e4m3fn).astype(np.float64)
    else:
        nib = np.empty((g, 128, n, 4), np.uint8)
        nib[..., 0::2] = words & 0xF
        nib[..., 1::2] = words >> 4
        vals = E2M1[nib]
    vals = vals * np.repeat(np.exp2(scales.astype(np.float64) - 127.0), 8, axis=1)[..., None]
    return vals.transpose(0, 1, 3, 2).reshape(g * 512, n)


def gelu(v):
    return 0.5 * v * (1.0 + np.tanh(np.sqrt(2.0 / np.pi) * (v + 0.044715 * v**3)))


K, H, N, T, S = 512, 1024, 768, 4096, 1024

def setup_inputs():
    n = np.random.standard_normal
    s = mx_kscale(K)[:, None]
    u = mx_kscale(H)[:, None]
    tab_words, tab_scales = pack_weight(n((K, T)) * s, "e2m1")
    offs = striped(np.random.permutation(T)[:S])
    offs2 = striped(np.random.permutation(T)[:S])
    w1 = (n((K, H)) / np.sqrt(K) / s).astype(np.float32)
    w2_words, w2_scales = pack_weight(n((K, H)) / np.sqrt(K) / s, "e4m3")
    bias = (0.5 * n(H)).astype(np.float32)
    gain = (1.5 * np.exp(0.3 * n(H)) * u[:, 0]).astype(np.float32)
    w3_words, w3_scales = pack_weight(n((H, N)) / np.sqrt(H) / u, "e2m1")
    hours = np.exp(0.4 * n((N, S))).astype(np.float32)
    sus = n((N, S)).astype(np.float32)
    return dict(tab_words=tab_words, tab_scales=tab_scales, offs=offs, offs2=offs2,
                w1=w1, w2_words=w2_words, w2_scales=w2_scales, bias=bias, gain=gain,
                w3_words=w3_words, w3_scales=w3_scales, hours=hours, sus=sus)

def reference(tab_words, tab_scales, offs, offs2, w1, w2_words, w2_scales, bias, gain,
              w3_words, w3_scales, hours, sus):
    TW = unpack_weight(tab_words, tab_scales, "e2m1")
    v = TW[:, unstriped(offs)]
    v2 = TW[:, unstriped(offs2)]
    w1q = mxq(f64(w1), 0, "e4m3")
    w2 = unpack_weight(w2_words, w2_scales, "e4m3")
    w3 = unpack_weight(w3_words, w3_scales, "e2m1")
    a = (w1q.T @ v + w2.T @ v2) + f64(bias)[:, None]
    h = f64(gain)[:, None] / (1.0 + np.exp(-a))
    hq = mxq(h, 0, "e4m3")
    y = w3.T @ hq
    return f64(sus) - f64(hours) * y

@@ -1,0 +1,223 @@
+from contextlib import ExitStack
+
+import concourse.mybir as mybir
+
+K, H, N, T, S = 512, 1024, 768, 4096, 1024
+FLOPS = 2 * K * H * S * 2 + 2 * H * N * S
+
+F32 = mybir.dt.float32
+BF16 = mybir.dt.bfloat16
+I32 = mybir.dt.int32
+U32 = mybir.dt.uint32
+U16 = mybir.dt.uint16
+U8 = mybir.dt.uint8
+FP8X4 = mybir.dt.float8_e4m3fn_x4
+FP4X4 = mybir.dt.float4_e2m1fn_x4
+ACT = mybir.ActivationFunctionType
+ALU = mybir.AluOpType
+
+P = 128
+HALF = 512
+BANK = 512
+NT = N // P
+CHUNKS = ((0, 512, "D", "AD"), (512, 256, "AA", "AA"), (768, 256, "AA", "AD"))
+QUART = 256
+
+
+def tile_list_measles_interchange_tracing_kernel(
+    tc, tab_words, tab_scales, offs, offs2, w1, w2_words, w2_scales, bias, gain,
+    w3_words, w3_scales, hours, sus, out,
+):
+    nc = tc.nc
+    with ExitStack() as ctx:
+        lists = ctx.enter_context(tc.tile_pool(name="lists", bufs=1))
+        keep = ctx.enter_context(tc.tile_pool(name="keep", bufs=1))
+        ring = ctx.enter_context(tc.tile_pool(name="ring", bufs=4))
+        res = ctx.enter_context(tc.tile_pool(name="res", bufs=6))
+        psum = ctx.enter_context(tc.psum_pool(name="psum", bufs=8))
+
+        def held(shape, dtype, name, tag=None):
+            return keep.tile(shape, dtype, name=name, tag=tag or name, align_bytes=64)
+
+        list_a = lists.tile([P, S // 16], U16, name="list_a")
+        list_b = lists.tile([P, S // 16], U16, name="list_b")
+        nc.sync.dma_start(list_a[:], offs)
+        nc.sync.dma_start(list_b[:], offs2)
+
+        table = held([P, T], U16, "table", "slot_a")
+        nc.sync.dma_start(table[:].bitcast(I32), tab_words[0].bitcast(I32))
+        warm_in = held([P, 1], F32, "warm_in", "slot_w0")
+        warm_out = held([P, 1], F32, "warm_out", "slot_w1")
+        warm_bias = held([P, 1], F32, "warm_bias", "slot_c")
+        warm_scale = held([P, 1], F32, "warm_scale", "slot_d")
+        warm_sum = held([P, 1], F32, "warm_sum", "slot_g")
+        for tile in (warm_in, warm_bias, warm_scale):
+            nc.vector.memset(tile[:], 0.0)
+        nc.scalar.activation(warm_out[:], warm_in[:], ACT.Sigmoid, bias=warm_bias[:], scale=warm_scale[:],
+                             accum_out=warm_sum[:])
+
+        table_sc = held([P, T], U8, "table_sc", "slot_h")
+        nc.vector.memset(table_sc[:].bitcast(I32), 0)
+        for q in range(4):
+            nc.sync.dma_start(table_sc[32 * q : 32 * q + 4, :].bitcast(I32),
+                              tab_scales[0, 4 * q : 4 * q + 4, :].bitcast(I32))
+
+        w1_rows = w1.rearrange("(p j) c -> p j c", j=4)
+        w1_raw = []
+
+        def load_w1(b):
+            w1_raw.append(held([P, 2, 4, QUART], F32, "w1_raw%d" % b, "slot_w%d" % b))
+            for u in range(2):
+                c0 = b * HALF + u * QUART
+                nc.sync.dma_start(w1_raw[b][:, u], w1_rows[:, :, c0 : c0 + QUART])
+
+        load_w1(0)
+        w2_raw = held([P, H], U32, "w2_raw", "slot_c")
+        nc.sync.dma_start(w2_raw[:].bitcast(I32), w2_words[0].rearrange("p c i -> p (c i)").bitcast(I32))
+        w2_sc_raw = held([P, H], U8, "w2_sc_raw", "slot_d")
+        nc.vector.memset(w2_sc_raw[:].bitcast(I32), 0)
+        for q in range(4):
+            nc.sync.dma_start(w2_sc_raw[32 * q : 32 * q + 4, :].bitcast(I32),
+                              w2_scales[0, 4 * q : 4 * q + 4, :].bitcast(I32))
+        load_w1(1)
+        consts = held([P, 2, 2, 4], F32, "consts", "slot_g")
+        bias_sb, gain_sb = consts[:, 0], consts[:, 1]
+        nc.sync.dma_start(bias_sb, bias.rearrange("(b p t) -> p b t", b=2, t=4))
+        nc.sync.dma_start(gain_sb, gain.rearrange("(b p t) -> p b t", b=2, t=4))
+
+        both = (list_a, list_b)
+        v_words, v_sc = {}, {}
+
+        def gather(store, window, dtype, k, half, tag=None):
+            store[k, half] = held([P, HALF], dtype, "v%d%d%d" % (dtype == U8, k, half), tag)
+            cols = slice(half * HALF // 16, (half + 1) * HALF // 16)
+            nc.vector.tensor_copy(store[k, half][:], window[:].indirect(both[k][:, cols]))
+
+        for k in range(2):
+            gather(v_words, table, U16, k, 0)
+        for k in range(2):
+            gather(v_sc, table_sc, U8, k, 0)
+
+        w2_codes = held([P, H], U32, "w2_codes")
+        w2_sc = held([P, H], U8, "w2_sc")
+        w1_codes = held([P, H], U32, "w1_codes")
+        w1_sc = held([P, H], U8, "w1_sc")
+        for b in range(2):
+            cols = slice(b * HALF, (b + 1) * HALF)
+            w1_bf = held([P, 4 * HALF], BF16, "w1_bf%d" % b, "slot_e%d" % b)
+            for u in range(2):
+                m = slice(u * QUART // 4, (u + 1) * QUART // 4)
+                nc.scalar.copy(w1_bf[:].rearrange("p (t m j) -> p m j t", t=4, j=4)[:, m],
+                               w1_raw[b][:, u].rearrange("p j (m t) -> p m j t", t=4))
+            nc.vector.quantize_mx(out=w1_codes[:, cols].bitcast(FP8X4), scales=w1_sc[:, cols], in_=w1_bf[:])
+            for dst, src in ((w2_codes, w2_raw), (w2_sc, w2_sc_raw)):
+                nc.vector.tensor_copy(dst[:, cols].rearrange("p (t m) -> p m t", t=4),
+                                      src[:, cols].rearrange("p (m t) -> p m t", t=4))
+
+        gather(v_sc, table_sc, U8, 0, 1, "slot_d")
+        gather(v_sc, table_sc, U8, 1, 1, "slot_w1")
+        v1 = held([P, 2, HALF], U16, "v_words1", "slot_e1")
+        for k in range(2):
+            v_words[k, 1] = v1[:, k]
+            nc.vector.tensor_copy(v1[:, k], table[:].indirect(both[k][:, HALF // 16 : S // 16]))
+
+        hours_sb, sus_sb = [], []
+        for half, tag in enumerate(("slot_w0", "slot_h")):
+            cols = slice(half * HALF, (half + 1) * HALF)
+            pair = held([P, 2, NT, HALF], F32, "pair%d" % half, tag)
+            hours_sb.append(pair[:, 0])
+            sus_sb.append(pair[:, 1])
+            nc.sync.dma_start(hours_sb[half], hours[:, cols].rearrange("(n p) j -> p n j", p=P))
+            nc.sync.dma_start(sus_sb[half], sus[:, cols].rearrange("(n p) j -> p n j", p=P))
+            if half == 0:
+                w3_sc = held([P, 2, N], U8, "w3_sc", "slot_e0")
+                nc.vector.memset(w3_sc[:].rearrange("p a c -> p (a c)").bitcast(I32), 0)
+                for q in range(4):
+                    nc.sync.dma_start(w3_sc[32 * q : 32 * q + 4, :, :].bitcast(I32),
+                                      w3_scales[:, 4 * q : 4 * q + 4, :].rearrange("a r c -> r a c").bitcast(I32))
+                w3_codes = held([P, 2, 2 * N], U8, "w3_codes", "slot_c")
+                nc.sync.dma_start(w3_codes[:].bitcast(I32), w3_words.rearrange("a p c -> p a c").bitcast(I32))
+
+        out_v = out.rearrange("(n p) j -> p n j", p=P)
+
+        def stage1(j0, width, b, mode):
+            half, c0 = divmod(j0, HALF)
+            step = HALF if width == HALF else P
+            per_bank = BANK // width
+            sig = ring.tile([P, 4, width], F32, name="sig")
+            if mode != "D":
+                h_rows = ring.tile([P, 4, width], BF16, name="h_rows")
+            accs = [psum.tile([P, per_bank, width], F32, name="acc") for t0 in range(0, 4, per_bank)]
+            passes = [(t, n0, k) for t in range(4) for n0 in range(0, width, step) for k in range(2)]
+            if width == HALF:
+                passes = [(t, 0, k) for k in range(2) for t in range(4)]
+            for t, n0, k in passes:
+                first = k == 0
+                k = (k + b) % 2
+                codes, scales = ((w1_codes, w1_sc), (w2_codes, w2_sc))[k]
+                wc = slice(b * HALF + t * P, b * HALF + (t + 1) * P)
+                nc.tensor.matmul_mx(
+                    out=accs[t // per_bank][:, t % per_bank, n0 : n0 + step],
+                    lhsT=codes[:, wc].bitcast(FP8X4), lhsT_scale=scales[:, wc],
+                    rhs=v_words[k, half][:, c0 + n0 : c0 + n0 + step].bitcast(FP4X4),
+                    rhs_scale=v_sc[k, half][:, c0 + n0 : c0 + n0 + step],
+                    start=first, stop=not first)
+            for t in range(4):
+                nc.scalar.activation(sig[:, t, :], accs[t // per_bank][:, t % per_bank, :], ACT.Sigmoid,
+                                     bias=bias_sb[:, b, t : t + 1])
+            if mode != "D":
+                for t in range(4):
+                    nc.scalar.activation(h_rows[:, t, :], sig[:, t, :], ACT.Copy, scale=gain_sb[:, b, t : t + 1])
+            h_bf = ring.tile([P, 4 * width], BF16, name="h_bf", align_bytes=64)
+            dst = h_bf[:].rearrange("p (c i t) -> p c t i", i=4, t=4)
+            if mode == "D":
+                nc.vector.tensor_tensor(
+                    dst, sig[:].rearrange("p t (c i) -> p c t i", i=4),
+                    gain_sb[:, b, :].unsqueeze(1).unsqueeze(3).to_broadcast([P, width // 4, 4, 4]), ALU.mult)
+            elif mode == "AD":
+                nc.vector.tensor_copy(dst, h_rows[:].rearrange("p t (c i) -> p c t i", i=4))
+            else:
+                nc.scalar.copy(dst, h_rows[:].rearrange("p t (c i) -> p c t i", i=4))
+            h_codes = held([P, width], U32, "h_codes_%d_%d" % (j0, b))
+            h_sc = held([P, width], U8, "h_sc_%d_%d" % (j0, b))
+            nc.vector.quantize_mx(out=h_codes[:].bitcast(FP8X4), scales=h_sc[:], in_=h_bf[:])
+            return h_codes, h_sc
+
+        late = []
+
+        def finish(prod, half, rows, cols, j0, width, per_bank):
+            score = res.tile([P, per_bank, width], F32, name="score")
+            nc.vector.tensor_tensor(score[:], sus_sb[half][:, rows, cols], prod[:], ALU.subtract)
+            nc.sync.dma_start(out_v[:, rows, j0 : j0 + width], score[:])
+
+        def stage2(j0, width, hq):
+            half, c0 = divmod(j0, HALF)
+            step = HALF if width == HALF else P
+            per_bank = min(BANK // width, 3)
+            for n0 in range(0, NT, per_bank):
+                acc = psum.tile([P, per_bank, width], F32, name="acc")
+                for n in range(n0, n0 + per_bank):
+                    for m0 in range(0, width, step):
+                        for b, (h_codes, h_sc) in enumerate(hq):
+                            nc.tensor.matmul_mx(
+                                out=acc[:, n - n0, m0 : m0 + step],
+                                lhsT=w3_codes[:, b, 2 * P * n : 2 * P * (n + 1)].bitcast(FP4X4),
+                                lhsT_scale=w3_sc[:, b, P * n : P * (n + 1)],
+                                rhs=h_codes[:, m0 : m0 + step].bitcast(FP8X4), rhs_scale=h_sc[:, m0 : m0 + step],
+                                start=(b == 0), stop=(b == 1))
+                rows = slice(n0, n0 + per_bank)
+                cols = slice(c0, c0 + width)
+                prod = res.tile([P, per_bank, width], F32, name="prod")
+                nc.vector.tensor_tensor(prod[:], acc[:], hours_sb[half][:, rows, cols], ALU.mult)
+                if late:
+                    finish(*late.pop())
+                late.append((prod, half, rows, cols, j0, width, per_bank))
+            finish(*late.pop())
+
+        pending = None
+        for j0, width, mode0, mode1 in CHUNKS:
+            hq = [stage1(j0, width, 0, mode0), stage1(j0, width, 1, mode1)]
+            if pending is not None:
+                stage2(*pending)
+            pending = (j0, width, hq)
+        stage2(*pending)

@@ -20,8 +20,10 @@ P = 128
 HALF = 512
 BANK = 512
 NT = N // P
-CHUNKS = ((0, 512, "D", "AD"), (512, 256, "AA", "AA"), (768, 256, "AA", "AD"))
+CHUNKS = ((0, 512, "AD", "D"), (512, 256, "AA", "AA"), (768, 256, "AD", "D"))
 QUART = 256
+LATE_BYTES = 64 * QUART + 5 * H + 64 + 6 * N + 8 * NT * S
+GP_UNITS = 1
 
 
 def tile_list_measles_interchange_tracing_kernel(
@@ -34,6 +36,7 @@ def tile_list_measles_interchange_tracing_kernel(
         keep = ctx.enter_context(tc.tile_pool(name="keep", bufs=1))
         ring = ctx.enter_context(tc.tile_pool(name="ring", bufs=4))
         res = ctx.enter_context(tc.tile_pool(name="res", bufs=6))
+        loads = ctx.enter_context(tc.tile_pool(name="loads", bufs=1))
         psum = ctx.enter_context(tc.psum_pool(name="psum", bufs=8))
 
         def held(shape, dtype, name, tag=None):
@@ -44,46 +47,65 @@ def tile_list_measles_interchange_tracing_kernel(
         nc.sync.dma_start(list_a[:], offs)
         nc.sync.dma_start(list_b[:], offs2)
 
-        table = held([P, T], U16, "table", "slot_a")
-        nc.sync.dma_start(table[:].bitcast(I32), tab_words[0].bitcast(I32))
-        warm_in = held([P, 1], F32, "warm_in", "slot_w0")
-        warm_out = held([P, 1], F32, "warm_out", "slot_w1")
-        warm_bias = held([P, 1], F32, "warm_bias", "slot_c")
-        warm_scale = held([P, 1], F32, "warm_scale", "slot_d")
-        warm_sum = held([P, 1], F32, "warm_sum", "slot_g")
-        for tile in (warm_in, warm_bias, warm_scale):
-            nc.vector.memset(tile[:], 0.0)
-        nc.scalar.activation(warm_out[:], warm_in[:], ACT.Sigmoid, bias=warm_bias[:], scale=warm_scale[:],
-                             accum_out=warm_sum[:])
-
-        table_sc = held([P, T], U8, "table_sc", "slot_h")
-        nc.vector.memset(table_sc[:].bitcast(I32), 0)
-        for q in range(4):
-            nc.sync.dma_start(table_sc[32 * q : 32 * q + 4, :].bitcast(I32),
-                              tab_scales[0, 4 * q : 4 * q + 4, :].bitcast(I32))
-
         w1_rows = w1.rearrange("(p j) c -> p j c", j=4)
-        w1_raw = []
 
-        def load_w1(b):
-            w1_raw.append(held([P, 2, 4, QUART], F32, "w1_raw%d" % b, "slot_w%d" % b))
-            for u in range(2):
-                c0 = b * HALF + u * QUART
-                nc.sync.dma_start(w1_raw[b][:, u], w1_rows[:, :, c0 : c0 + QUART])
+        def load_scale_rows(plane, rows):
+            for q in (0, 2, 1, 3):
+                nc.sync.dma_start(plane[32 * q : 32 * q + 4].bitcast(I32), rows[4 * q : 4 * q + 4].bitcast(I32))
+
+        table = held([P, T], U16, "table")
+        nc.sync.dma_start(table[:].bitcast(I32), tab_words[0].bitcast(I32))
+
+        table_sc = held([P, T], U8, "table_sc")
+        nc.vector.memset(table_sc[:].bitcast(I32), 0)
+        load_scale_rows(table_sc, tab_scales[0])
+
+        place = [0]
+
+        def late_tile(shape, dtype, name, size):
+            tile = loads.tile(shape, dtype, name=name, offset=place[0], align_bytes=64)
+            place[0] = place[0] + size
+            return tile
+
+        warm_in = held([P, 640], F32, "warm_in")
+        gate = loads.tile([P, LATE_BYTES // 4], F32, name="gate", offset=0, align_bytes=64)
+        nc.gpsimd.memset(warm_in[:], 0.0)
+        nc.scalar.activation(gate[:, 0:640], warm_in[:], ACT.Sigmoid)
+
+        w1_raw, w1_place = [], []
+
+        def load_w1(piece):
+            w1_place.append(place[0])
+            w1_raw.append(late_tile([P, 4, QUART], F32, "w1_raw%d" % piece, 16 * QUART))
+            nc.sync.dma_start(w1_raw[piece][:], w1_rows[:, :, piece * QUART : (piece + 1) * QUART])
 
         load_w1(0)
-        w2_raw = held([P, H], U32, "w2_raw", "slot_c")
-        nc.sync.dma_start(w2_raw[:].bitcast(I32), w2_words[0].rearrange("p c i -> p (c i)").bitcast(I32))
-        w2_sc_raw = held([P, H], U8, "w2_sc_raw", "slot_d")
-        nc.vector.memset(w2_sc_raw[:].bitcast(I32), 0)
-        for q in range(4):
-            nc.sync.dma_start(w2_sc_raw[32 * q : 32 * q + 4, :].bitcast(I32),
-                              w2_scales[0, 4 * q : 4 * q + 4, :].bitcast(I32))
         load_w1(1)
-        consts = held([P, 2, 2, 4], F32, "consts", "slot_g")
+        w2_raw = late_tile([P, H], U32, "w2_raw", 4 * H)
+        nc.sync.dma_start(w2_raw[:].bitcast(I32), w2_words[0].rearrange("p c i -> p (c i)").bitcast(I32))
+        w2_sc_place = place[0]
+        w2_sc_raw = late_tile([P, H], U8, "w2_sc_raw", H)
+        nc.vector.memset(w2_sc_raw[:].bitcast(I32), 0)
+        load_scale_rows(w2_sc_raw, w2_scales[0])
+        load_w1(2)
+        load_w1(3)
+        consts = late_tile([P, 2, 2, 4], F32, "consts", 64)
         bias_sb, gain_sb = consts[:, 0], consts[:, 1]
         nc.sync.dma_start(bias_sb, bias.rearrange("(b p t) -> p b t", b=2, t=4))
         nc.sync.dma_start(gain_sb, gain.rearrange("(b p t) -> p b t", b=2, t=4))
+
+        given = {}
+        for g in range(NT // 2):
+            for x, src in enumerate((hours, sus)):
+                given[x, g] = late_tile([P, 2, S], F32, "given%d%d" % (x, g), 8 * S)
+                nc.sync.dma_start(given[x, g][:], src.rearrange("(n p) j -> p n j", p=P)[:, 2 * g : 2 * g + 2, :])
+            if g == 0:
+                w3_sc = late_tile([P, 2, N], U8, "w3_sc", 2 * N)
+                nc.vector.memset(w3_sc[:].rearrange("p a c -> p (a c)").bitcast(I32), 0)
+                load_scale_rows(w3_sc, w3_scales.rearrange("a r c -> r a c"))
+                w3_codes = late_tile([P, 2, 2 * N], U8, "w3_codes", 4 * N)
+                nc.sync.dma_start(w3_codes[:].bitcast(I32), w3_words.rearrange("a p c -> p a c").bitcast(I32))
+        assert place[0] == LATE_BYTES
 
         both = (list_a, list_b)
         v_words, v_sc = {}, {}
@@ -105,38 +127,22 @@ def tile_list_measles_interchange_tracing_kernel(
         for b in range(2):
             cols = slice(b * HALF, (b + 1) * HALF)
             w1_bf = held([P, 4 * HALF], BF16, "w1_bf%d" % b, "slot_e%d" % b)
-            for u in range(2):
-                m = slice(u * QUART // 4, (u + 1) * QUART // 4)
-                nc.scalar.copy(w1_bf[:].rearrange("p (t m j) -> p m j t", t=4, j=4)[:, m],
-                               w1_raw[b][:, u].rearrange("p j (m t) -> p m j t", t=4))
+            pieces = ((0, w1_raw[2 * b]), (QUART // 4, w1_raw[2 * b + 1]))
+            for m0, raw in pieces:
+                src = raw[:].rearrange("p j (m t) -> p m j t", t=4)
+                nc.scalar.copy(w1_bf[:].rearrange("p (t m j) -> p m j t", t=4, j=4)[:, m0 : m0 + src.shape[1]], src)
             nc.vector.quantize_mx(out=w1_codes[:, cols].bitcast(FP8X4), scales=w1_sc[:, cols], in_=w1_bf[:])
             for dst, src in ((w2_codes, w2_raw), (w2_sc, w2_sc_raw)):
                 nc.vector.tensor_copy(dst[:, cols].rearrange("p (t m) -> p m t", t=4),
                                       src[:, cols].rearrange("p (m t) -> p m t", t=4))
 
-        gather(v_sc, table_sc, U8, 0, 1, "slot_d")
-        gather(v_sc, table_sc, U8, 1, 1, "slot_w1")
+        for k, spot in enumerate((w2_sc_place, w1_place[3])):
+            v_sc[k, 1] = loads.tile([P, HALF], U8, name="sc_late%d" % k, offset=spot, align_bytes=64)
+            nc.vector.tensor_copy(v_sc[k, 1][:], table_sc[:].indirect(both[k][:, HALF // 16 : S // 16]))
         v1 = held([P, 2, HALF], U16, "v_words1", "slot_e1")
         for k in range(2):
             v_words[k, 1] = v1[:, k]
             nc.vector.tensor_copy(v1[:, k], table[:].indirect(both[k][:, HALF // 16 : S // 16]))
-
-        hours_sb, sus_sb = [], []
-        for half, tag in enumerate(("slot_w0", "slot_h")):
-            cols = slice(half * HALF, (half + 1) * HALF)
-            pair = held([P, 2, NT, HALF], F32, "pair%d" % half, tag)
-            hours_sb.append(pair[:, 0])
-            sus_sb.append(pair[:, 1])
-            nc.sync.dma_start(hours_sb[half], hours[:, cols].rearrange("(n p) j -> p n j", p=P))
-            nc.sync.dma_start(sus_sb[half], sus[:, cols].rearrange("(n p) j -> p n j", p=P))
-            if half == 0:
-                w3_sc = held([P, 2, N], U8, "w3_sc", "slot_e0")
-                nc.vector.memset(w3_sc[:].rearrange("p a c -> p (a c)").bitcast(I32), 0)
-                for q in range(4):
-                    nc.sync.dma_start(w3_sc[32 * q : 32 * q + 4, :, :].bitcast(I32),
-                                      w3_scales[:, 4 * q : 4 * q + 4, :].rearrange("a r c -> r a c").bitcast(I32))
-                w3_codes = held([P, 2, 2 * N], U8, "w3_codes", "slot_c")
-                nc.sync.dma_start(w3_codes[:].bitcast(I32), w3_words.rearrange("a p c -> p a c").bitcast(I32))
 
         out_v = out.rearrange("(n p) j -> p n j", p=P)
 
@@ -165,8 +171,10 @@ def tile_list_measles_interchange_tracing_kernel(
             for t in range(4):
                 nc.scalar.activation(sig[:, t, :], accs[t // per_bank][:, t % per_bank, :], ACT.Sigmoid,
                                      bias=bias_sb[:, b, t : t + 1])
-            if mode != "D":
-                for t in range(4):
+            for t in range(4):
+                if mode == "DD":
+                    nc.vector.tensor_scalar(h_rows[:, t, :], sig[:, t, :], gain_sb[:, b, t : t + 1], None, ALU.mult)
+                elif mode != "D":
                     nc.scalar.activation(h_rows[:, t, :], sig[:, t, :], ACT.Copy, scale=gain_sb[:, b, t : t + 1])
             h_bf = ring.tile([P, 4 * width], BF16, name="h_bf", align_bytes=64)
             dst = h_bf[:].rearrange("p (c i t) -> p c t i", i=4, t=4)
@@ -174,7 +182,7 @@ def tile_list_measles_interchange_tracing_kernel(
                 nc.vector.tensor_tensor(
                     dst, sig[:].rearrange("p t (c i) -> p c t i", i=4),
                     gain_sb[:, b, :].unsqueeze(1).unsqueeze(3).to_broadcast([P, width // 4, 4, 4]), ALU.mult)
-            elif mode == "AD":
+            elif mode != "AA":
                 nc.vector.tensor_copy(dst, h_rows[:].rearrange("p t (c i) -> p c t i", i=4))
             else:
                 nc.scalar.copy(dst, h_rows[:].rearrange("p t (c i) -> p c t i", i=4))
@@ -183,36 +191,41 @@ def tile_list_measles_interchange_tracing_kernel(
             nc.vector.quantize_mx(out=h_codes[:].bitcast(FP8X4), scales=h_sc[:], in_=h_bf[:])
             return h_codes, h_sc
 
-        late = []
-
-        def finish(prod, half, rows, cols, j0, width, per_bank):
-            score = res.tile([P, per_bank, width], F32, name="score")
-            nc.vector.tensor_tensor(score[:], sus_sb[half][:, rows, cols], prod[:], ALU.subtract)
-            nc.sync.dma_start(out_v[:, rows, j0 : j0 + width], score[:])
-
         def stage2(j0, width, hq):
             half, c0 = divmod(j0, HALF)
             step = HALF if width == HALF else P
             per_bank = min(BANK // width, 3)
-            for n0 in range(0, NT, per_bank):
-                acc = psum.tile([P, per_bank, width], F32, name="acc")
-                for n in range(n0, n0 + per_bank):
-                    for m0 in range(0, width, step):
-                        for b, (h_codes, h_sc) in enumerate(hq):
-                            nc.tensor.matmul_mx(
-                                out=acc[:, n - n0, m0 : m0 + step],
-                                lhsT=w3_codes[:, b, 2 * P * n : 2 * P * (n + 1)].bitcast(FP4X4),
-                                lhsT_scale=w3_sc[:, b, P * n : P * (n + 1)],
-                                rhs=h_codes[:, m0 : m0 + step].bitcast(FP8X4), rhs_scale=h_sc[:, m0 : m0 + step],
-                                start=(b == 0), stop=(b == 1))
-                rows = slice(n0, n0 + per_bank)
-                cols = slice(c0, c0 + width)
-                prod = res.tile([P, per_bank, width], F32, name="prod")
-                nc.vector.tensor_tensor(prod[:], acc[:], hours_sb[half][:, rows, cols], ALU.mult)
-                if late:
-                    finish(*late.pop())
-                late.append((prod, half, rows, cols, j0, width, per_bank))
-            finish(*late.pop())
+            accs = [psum.tile([P, per_bank, width], F32, name="acc") for n0 in range(0, NT, per_bank)]
+
+            def passes(bank, b):
+                h_codes, h_sc = hq[b]
+                spots = [(n, m0) for n in range(per_bank) for m0 in range(0, width, step)]
+                for i, (u, m0) in enumerate(spots):
+                    n = bank * per_bank + u
+                    nc.tensor.matmul_mx(
+                        out=accs[bank][:, u, m0 : m0 + step],
+                        lhsT=w3_codes[:, b, 2 * P * n : 2 * P * (n + 1)].bitcast(FP4X4),
+                        lhsT_scale=w3_sc[:, b, P * n : P * (n + 1)],
+                        rhs=h_codes[:, m0 : m0 + step].bitcast(FP8X4), rhs_scale=h_sc[:, m0 : m0 + step],
+                        start=(b == 0 and i == 0), stop=(b == 1 and i == len(spots) - 1))
+
+            ahead = min(4, len(accs))
+            for bank in range(ahead):
+                passes(bank, 0)
+            cols = slice(j0, j0 + width)
+            prods = [res.tile([P, 2, width], F32, name="prod") for g in range(NT // 2)]
+            for bank, n0 in enumerate(range(0, NT, per_bank)):
+                if bank >= ahead:
+                    passes(bank, 0)
+                passes(bank, 1)
+                g, u = divmod(n0, 2)
+                rows = slice(u, u + per_bank)
+                nc.vector.tensor_tensor(prods[g][:, rows], accs[bank][:], given[0, g][:, rows, cols], ALU.mult)
+            for g in range(NT // 2):
+                score = res.tile([P, 2, width], F32, name="score")
+                engine = nc.gpsimd if g < GP_UNITS else nc.vector
+                engine.tensor_tensor(score[:], given[1, g][:, :, cols], prods[g][:], ALU.subtract)
+                nc.sync.dma_start(out_v[:, 2 * g : 2 * g + 2, cols], score[:])
 
         pending = None
         for j0, width, mode0, mode1 in CHUNKS:

@@ -20,7 +20,7 @@ P = 128
 HALF = 512
 BANK = 512
 NT = N // P
-CHUNKS = ((0, 512, "AD", "D"), (512, 256, "AA", "AA"), (768, 256, "AD", "D"))
+CHUNKS = ((0, 512, "AD", "D"), (512, 256, "AA", "AA"), (768, 256, "AA", "AD"))
 QUART = 256
 LATE_BYTES = 64 * QUART + 5 * H + 64 + 6 * N + 8 * NT * S
 GP_UNITS = 1
@@ -95,16 +95,22 @@ def tile_list_measles_interchange_tracing_kernel(
         nc.sync.dma_start(gain_sb, gain.rearrange("(b p t) -> p b t", b=2, t=4))
 
         given = {}
-        for g in range(NT // 2):
-            for x, src in enumerate((hours, sus)):
-                given[x, g] = late_tile([P, 2, S], F32, "given%d%d" % (x, g), 8 * S)
-                nc.sync.dma_start(given[x, g][:], src.rearrange("(n p) j -> p n j", p=P)[:, 2 * g : 2 * g + 2, :])
-            if g == 0:
-                w3_sc = late_tile([P, 2, N], U8, "w3_sc", 2 * N)
-                nc.vector.memset(w3_sc[:].rearrange("p a c -> p (a c)").bitcast(I32), 0)
-                load_scale_rows(w3_sc, w3_scales.rearrange("a r c -> r a c"))
-                w3_codes = late_tile([P, 2, 2 * N], U8, "w3_codes", 4 * N)
-                nc.sync.dma_start(w3_codes[:].bitcast(I32), w3_words.rearrange("a p c -> p a c").bitcast(I32))
+
+        def load_given(x, g):
+            given[x, g] = late_tile([P, 2, S], F32, "given%d%d" % (x, g), 8 * S)
+            rows = (hours, sus)[x].rearrange("(n p) j -> p n j", p=P)
+            nc.sync.dma_start(given[x, g][:], rows[:, 2 * g : 2 * g + 2, :])
+
+        load_given(0, 0)
+        load_given(1, 0)
+        w3_sc = late_tile([P, 2, N], U8, "w3_sc", 2 * N)
+        nc.vector.memset(w3_sc[:].rearrange("p a c -> p (a c)").bitcast(I32), 0)
+        load_scale_rows(w3_sc, w3_scales.rearrange("a r c -> r a c"))
+        w3_codes = late_tile([P, 2, 2 * N], U8, "w3_codes", 4 * N)
+        nc.sync.dma_start(w3_codes[:].bitcast(I32), w3_words.rearrange("a p c -> p a c").bitcast(I32))
+        for x in range(2):
+            for g in range(1, NT // 2):
+                load_given(x, g)
         assert place[0] == LATE_BYTES
 
         both = (list_a, list_b)
@@ -117,8 +123,10 @@ def tile_list_measles_interchange_tracing_kernel(
 
         for k in range(2):
             gather(v_words, table, U16, k, 0)
-        for k in range(2):
-            gather(v_sc, table_sc, U8, k, 0)
+        sc_a = held([P, S], U8, "sc_a")
+        nc.vector.tensor_copy(sc_a[:], table_sc[:].indirect(list_a[:]))
+        v_sc[0, 0], v_sc[0, 1] = sc_a[:, 0:HALF], sc_a[:, HALF:S]
+        gather(v_sc, table_sc, U8, 1, 0)
 
         w2_codes = held([P, H], U32, "w2_codes")
         w2_sc = held([P, H], U8, "w2_sc")
@@ -136,9 +144,8 @@ def tile_list_measles_interchange_tracing_kernel(
                 nc.vector.tensor_copy(dst[:, cols].rearrange("p (t m) -> p m t", t=4),
                                       src[:, cols].rearrange("p (m t) -> p m t", t=4))
 
-        for k, spot in enumerate((w2_sc_place, w1_place[3])):
-            v_sc[k, 1] = loads.tile([P, HALF], U8, name="sc_late%d" % k, offset=spot, align_bytes=64)
-            nc.vector.tensor_copy(v_sc[k, 1][:], table_sc[:].indirect(both[k][:, HALF // 16 : S // 16]))
+        v_sc[1, 1] = loads.tile([P, HALF], U8, name="sc_late", offset=w1_place[3], align_bytes=64)
+        nc.vector.tensor_copy(v_sc[1, 1][:], table_sc[:].indirect(list_b[:, HALF // 16 : S // 16]))
         v1 = held([P, 2, HALF], U16, "v_words1", "slot_e1")
         for k in range(2):
             v_words[k, 1] = v1[:, k]

@@ -1,6 +1,7 @@
 from contextlib import ExitStack
 
 import concourse.mybir as mybir
+from concourse.masks import make_identity
 
 K, H, N, T, S = 512, 1024, 768, 4096, 1024
 FLOPS = 2 * K * H * S * 2 + 2 * H * N * S
@@ -18,12 +19,11 @@ ALU = mybir.AluOpType
 
 P = 128
 HALF = 512
-BANK = 512
-NT = N // P
-CHUNKS = ((0, 512, "AD", "D"), (512, 256, "AA", "AA"), (768, 256, "AA", "AD"))
 QUART = 256
-LATE_BYTES = 64 * QUART + 5 * H + 64 + 6 * N + 8 * NT * S
-GP_UNITS = 1
+PAIRS = N // (2 * P)
+W1_RAW_AT = 0
+W2_SC_AT = 4 * 16 * QUART
+W1_BF_AT = W2_SC_AT + H
 
 
 def tile_list_measles_interchange_tracing_kernel(
@@ -35,178 +35,171 @@ def tile_list_measles_interchange_tracing_kernel(
         lists = ctx.enter_context(tc.tile_pool(name="lists", bufs=1))
         keep = ctx.enter_context(tc.tile_pool(name="keep", bufs=1))
         ring = ctx.enter_context(tc.tile_pool(name="ring", bufs=4))
+        shared = ctx.enter_context(tc.tile_pool(name="shared", bufs=1))
         res = ctx.enter_context(tc.tile_pool(name="res", bufs=6))
-        loads = ctx.enter_context(tc.tile_pool(name="loads", bufs=1))
-        psum = ctx.enter_context(tc.psum_pool(name="psum", bufs=8))
+        psum_consts = ctx.enter_context(tc.psum_pool(name="psum_consts", bufs=1))
+        psum = ctx.enter_context(tc.psum_pool(name="psum", bufs=7))
 
         def held(shape, dtype, name, tag=None):
             return keep.tile(shape, dtype, name=name, tag=tag or name, align_bytes=64)
+
+        def placed(shape, dtype, name, offset):
+            return shared.tile(shape, dtype, name=name, offset=offset, align_bytes=64)
 
         list_a = lists.tile([P, S // 16], U16, name="list_a")
         list_b = lists.tile([P, S // 16], U16, name="list_b")
         nc.sync.dma_start(list_a[:], offs)
         nc.sync.dma_start(list_b[:], offs2)
-
-        w1_rows = w1.rearrange("(p j) c -> p j c", j=4)
+        both = (list_a, list_b)
 
         def load_scale_rows(plane, rows):
-            for q in (0, 2, 1, 3):
-                nc.sync.dma_start(plane[32 * q : 32 * q + 4].bitcast(I32), rows[4 * q : 4 * q + 4].bitcast(I32))
+            for r in range(4):
+                nc.sync.dma_start(plane[r:P:32].bitcast(I32), rows[r:16:4].bitcast(I32))
 
         table = held([P, T], U16, "table")
+        table_sc = held([P, T], U8, "table_sc")
+        nc.vector.memset(table_sc[:, 0 : T // 2].bitcast(I32), 0)
+        nc.gpsimd.memset(table_sc[:, T // 2 : T].bitcast(I32), 0)
+        load_scale_rows(table_sc, tab_scales[0])
         nc.sync.dma_start(table[:].bitcast(I32), tab_words[0].bitcast(I32))
 
-        table_sc = held([P, T], U8, "table_sc")
-        nc.vector.memset(table_sc[:].bitcast(I32), 0)
-        load_scale_rows(table_sc, tab_scales[0])
+        w2_sc_raw = placed([P, H], U8, "w2_sc_raw", W2_SC_AT)
+        nc.vector.memset(w2_sc_raw[:].bitcast(I32), 0)
+        w3_sc = held([P, 2, N], U8, "w3_sc")
+        nc.vector.memset(w3_sc[:].rearrange("p a c -> p (a c)").bitcast(I32), 0)
+        const_rows = held([P, HALF], F32, "const_rows")
+        nc.gpsimd.memset(const_rows[:], 0.0)
+        identity = held([P, P], F32, "identity")
+        make_identity(nc, identity[:])
+        warm_out = held([P, 8], F32, "warm_out")
+        nc.scalar.activation(warm_out[:, 0:1], identity[:, 0:1], ACT.Sigmoid)
 
-        place = [0]
-
-        def late_tile(shape, dtype, name, size):
-            tile = loads.tile(shape, dtype, name=name, offset=place[0], align_bytes=64)
-            place[0] = place[0] + size
-            return tile
-
-        warm_in = held([P, 640], F32, "warm_in")
-        gate = loads.tile([P, LATE_BYTES // 4], F32, name="gate", offset=0, align_bytes=64)
-        nc.gpsimd.memset(warm_in[:], 0.0)
-        nc.scalar.activation(gate[:, 0:640], warm_in[:], ACT.Sigmoid)
-
-        w1_raw, w1_place = [], []
+        w1_rows = w1.rearrange("(p j) c -> p j c", j=4)
+        w2_flat = w2_words[0].rearrange("p c i -> p (c i)").bitcast(I32)
+        w1_raw, w2_raw = [], []
 
         def load_w1(piece):
-            w1_place.append(place[0])
-            w1_raw.append(late_tile([P, 4, QUART], F32, "w1_raw%d" % piece, 16 * QUART))
+            w1_raw.append(placed([P, 4, QUART], F32, "w1_raw%d" % piece, W1_RAW_AT + 16 * QUART * piece))
             nc.sync.dma_start(w1_raw[piece][:], w1_rows[:, :, piece * QUART : (piece + 1) * QUART])
+
+        def load_w2(b):
+            w2_raw.append(held([P, HALF], U32, "w2_raw%d" % b))
+            nc.sync.dma_start(w2_raw[b][:].bitcast(I32), w2_flat[:, b * HALF : (b + 1) * HALF])
 
         load_w1(0)
         load_w1(1)
-        w2_raw = late_tile([P, H], U32, "w2_raw", 4 * H)
-        nc.sync.dma_start(w2_raw[:].bitcast(I32), w2_words[0].rearrange("p c i -> p (c i)").bitcast(I32))
-        w2_sc_place = place[0]
-        w2_sc_raw = late_tile([P, H], U8, "w2_sc_raw", H)
-        nc.vector.memset(w2_sc_raw[:].bitcast(I32), 0)
+        nc.sync.dma_start(const_rows[0:2, :], gain.rearrange("(b c) -> b c", b=2))
+        nc.sync.dma_start(const_rows[2:4, :], bias.rearrange("(b c) -> b c", b=2))
+        load_w2(0)
         load_scale_rows(w2_sc_raw, w2_scales[0])
         load_w1(2)
         load_w1(3)
-        consts = late_tile([P, 2, 2, 4], F32, "consts", 64)
-        bias_sb, gain_sb = consts[:, 0], consts[:, 1]
-        nc.sync.dma_start(bias_sb, bias.rearrange("(b p t) -> p b t", b=2, t=4))
-        nc.sync.dma_start(gain_sb, gain.rearrange("(b p t) -> p b t", b=2, t=4))
-
+        load_w2(1)
+        load_scale_rows(w3_sc, w3_scales.rearrange("a r c -> r a c"))
+        w3_codes = held([P, 2, 2 * N], U8, "w3_codes")
+        nc.sync.dma_start(w3_codes[:].bitcast(I32), w3_words.rearrange("a p c -> p a c").bitcast(I32))
         given = {}
-
-        def load_given(x, g):
-            given[x, g] = late_tile([P, 2, S], F32, "given%d%d" % (x, g), 8 * S)
+        for x, g in ((0, 0), (0, 1), (0, 2), (1, 0), (1, 1), (1, 2)):
+            given[x, g] = held([P, 2, S], F32, "given%d%d" % (x, g))
             rows = (hours, sus)[x].rearrange("(n p) j -> p n j", p=P)
             nc.sync.dma_start(given[x, g][:], rows[:, 2 * g : 2 * g + 2, :])
 
-        load_given(0, 0)
-        load_given(1, 0)
-        w3_sc = late_tile([P, 2, N], U8, "w3_sc", 2 * N)
-        nc.vector.memset(w3_sc[:].rearrange("p a c -> p (a c)").bitcast(I32), 0)
-        load_scale_rows(w3_sc, w3_scales.rearrange("a r c -> r a c"))
-        w3_codes = late_tile([P, 2, 2 * N], U8, "w3_codes", 4 * N)
-        nc.sync.dma_start(w3_codes[:].bitcast(I32), w3_words.rearrange("a p c -> p a c").bitcast(I32))
-        for x in range(2):
-            for g in range(1, NT // 2):
-                load_given(x, g)
-        assert place[0] == LATE_BYTES
+        consts_ps = psum_consts.tile([P, 4, P], F32, name="consts_ps")
+        for t in range(4):
+            nc.tensor.transpose(consts_ps[:, t, :], const_rows[:, t:HALF:4], identity[:])
+        consts = held([P, 4, 4], F32, "consts")
+        nc.scalar.copy(consts[:], consts_ps[:, :, 0:4])
 
-        both = (list_a, list_b)
         v_words, v_sc = {}, {}
 
-        def gather(store, window, dtype, k, half, tag=None):
-            store[k, half] = held([P, HALF], dtype, "v%d%d%d" % (dtype == U8, k, half), tag)
+        def gather(store, window, k, half, dst):
             cols = slice(half * HALF // 16, (half + 1) * HALF // 16)
-            nc.vector.tensor_copy(store[k, half][:], window[:].indirect(both[k][:, cols]))
+            store[k, half] = dst[:]
+            nc.vector.tensor_copy(dst[:], window[:].indirect(both[k][:, cols]))
 
         for k in range(2):
-            gather(v_words, table, U16, k, 0)
-        sc_a = held([P, S], U8, "sc_a")
-        nc.vector.tensor_copy(sc_a[:], table_sc[:].indirect(list_a[:]))
-        v_sc[0, 0], v_sc[0, 1] = sc_a[:, 0:HALF], sc_a[:, HALF:S]
-        gather(v_sc, table_sc, U8, 1, 0)
+            gather(v_sc, table_sc, k, 0, held([P, HALF], U8, "sc0_%d" % k))
+        for k in range(2):
+            gather(v_words, table, k, 0, held([P, HALF], U16, "words0_%d" % k))
 
-        w2_codes = held([P, H], U32, "w2_codes")
-        w2_sc = held([P, H], U8, "w2_sc")
-        w1_codes = held([P, H], U32, "w1_codes")
-        w1_sc = held([P, H], U8, "w1_sc")
-        for b in range(2):
+        w_codes = [held([P, H], U32, "w%d_codes" % k) for k in (1, 2)]
+        w_sc = [held([P, H], U8, "w%d_sc" % k) for k in (1, 2)]
+
+        def deal(dst, src):
+            nc.vector.tensor_copy(dst.rearrange("p (b t m) -> p b m t", t=4, m=P),
+                                  src.rearrange("p (b m t) -> p b m t", t=4, m=P))
+
+        def prepare_weights(b):
             cols = slice(b * HALF, (b + 1) * HALF)
-            w1_bf = held([P, 4 * HALF], BF16, "w1_bf%d" % b, "slot_e%d" % b)
-            pieces = ((0, w1_raw[2 * b]), (QUART // 4, w1_raw[2 * b + 1]))
-            for m0, raw in pieces:
-                src = raw[:].rearrange("p j (m t) -> p m j t", t=4)
-                nc.scalar.copy(w1_bf[:].rearrange("p (t m j) -> p m j t", t=4, j=4)[:, m0 : m0 + src.shape[1]], src)
-            nc.vector.quantize_mx(out=w1_codes[:, cols].bitcast(FP8X4), scales=w1_sc[:, cols], in_=w1_bf[:])
-            for dst, src in ((w2_codes, w2_raw), (w2_sc, w2_sc_raw)):
-                nc.vector.tensor_copy(dst[:, cols].rearrange("p (t m) -> p m t", t=4),
-                                      src[:, cols].rearrange("p (m t) -> p m t", t=4))
+            w1_bf = placed([P, 4 * HALF], BF16, "w1_bf%d" % b, W1_BF_AT + 8 * HALF * b)
+            dealt = w1_bf[:].rearrange("p (t m j) -> p m j t", t=4, j=4)
+            for piece in range(2):
+                src = w1_raw[2 * b + piece][:].rearrange("p j (m t) -> p m j t", t=4)
+                nc.scalar.copy(dealt[:, piece * QUART // 4 : (piece + 1) * QUART // 4], src)
+            deal(w_codes[1][:, cols], w2_raw[b][:])
+            nc.vector.quantize_mx(out=w_codes[0][:, cols].bitcast(FP8X4), scales=w_sc[0][:, cols], in_=w1_bf[:])
 
-        v_sc[1, 1] = loads.tile([P, HALF], U8, name="sc_late", offset=w1_place[3], align_bytes=64)
-        nc.vector.tensor_copy(v_sc[1, 1][:], table_sc[:].indirect(list_b[:, HALF // 16 : S // 16]))
-        v1 = held([P, 2, HALF], U16, "v_words1", "slot_e1")
-        for k in range(2):
-            v_words[k, 1] = v1[:, k]
-            nc.vector.tensor_copy(v1[:, k], table[:].indirect(both[k][:, HALF // 16 : S // 16]))
+        prepare_weights(0)
+        gather(v_sc, table_sc, 0, 1, placed([P, HALF], U8, "sc1_0", W1_RAW_AT))
+        deal(w_sc[1][:], w2_sc_raw[:])
+        gather(v_sc, table_sc, 1, 1, placed([P, HALF], U8, "sc1_1", W2_SC_AT))
+        gather(v_words, table, 0, 1, placed([P, HALF], U16, "words1_0", W2_SC_AT + HALF))
+        prepare_weights(1)
+        gather(v_words, table, 1, 1, placed([P, HALF], U16, "words1_1", W1_BF_AT + 8 * HALF))
 
-        out_v = out.rearrange("(n p) j -> p n j", p=P)
+        def first_product(half, b, sig=None):
+            if sig is None:
+                sig = ring.tile([P, 4, HALF], F32, name="sig")
+            accs = [psum.tile([P, HALF], F32, name="acc") for t in range(4)]
 
-        def stage1(j0, width, b, mode):
-            half, c0 = divmod(j0, HALF)
-            step = HALF if width == HALF else P
-            per_bank = BANK // width
-            sig = ring.tile([P, 4, width], F32, name="sig")
-            if mode != "D":
-                h_rows = ring.tile([P, 4, width], BF16, name="h_rows")
-            accs = [psum.tile([P, per_bank, width], F32, name="acc") for t0 in range(0, 4, per_bank)]
-            passes = [(t, n0, k) for t in range(4) for n0 in range(0, width, step) for k in range(2)]
-            if width == HALF:
-                passes = [(t, 0, k) for k in range(2) for t in range(4)]
-            for t, n0, k in passes:
-                first = k == 0
-                k = (k + b) % 2
-                codes, scales = ((w1_codes, w1_sc), (w2_codes, w2_sc))[k]
+            def one_pass(t, k, first):
                 wc = slice(b * HALF + t * P, b * HALF + (t + 1) * P)
                 nc.tensor.matmul_mx(
-                    out=accs[t // per_bank][:, t % per_bank, n0 : n0 + step],
-                    lhsT=codes[:, wc].bitcast(FP8X4), lhsT_scale=scales[:, wc],
-                    rhs=v_words[k, half][:, c0 + n0 : c0 + n0 + step].bitcast(FP4X4),
-                    rhs_scale=v_sc[k, half][:, c0 + n0 : c0 + n0 + step],
-                    start=first, stop=not first)
+                    out=accs[t][:], lhsT=w_codes[k][:, wc].bitcast(FP8X4), lhsT_scale=w_sc[k][:, wc],
+                    rhs=v_words[k, half].bitcast(FP4X4), rhs_scale=v_sc[k, half], start=first, stop=not first)
+
             for t in range(4):
-                nc.scalar.activation(sig[:, t, :], accs[t // per_bank][:, t % per_bank, :], ACT.Sigmoid,
-                                     bias=bias_sb[:, b, t : t + 1])
+                one_pass(t, b, True)
             for t in range(4):
-                if mode == "DD":
-                    nc.vector.tensor_scalar(h_rows[:, t, :], sig[:, t, :], gain_sb[:, b, t : t + 1], None, ALU.mult)
-                elif mode != "D":
-                    nc.scalar.activation(h_rows[:, t, :], sig[:, t, :], ACT.Copy, scale=gain_sb[:, b, t : t + 1])
+                one_pass(t, 1 - b, False)
+                nc.scalar.activation(sig[:, t, :], accs[t][:], ACT.Sigmoid, bias=consts[:, t, 2 + b : 3 + b])
+            return sig
+
+        def gain_on_vector(sig, b, c0, width):
             h_bf = ring.tile([P, 4 * width], BF16, name="h_bf", align_bytes=64)
-            dst = h_bf[:].rearrange("p (c i t) -> p c t i", i=4, t=4)
-            if mode == "D":
-                nc.vector.tensor_tensor(
-                    dst, sig[:].rearrange("p t (c i) -> p c t i", i=4),
-                    gain_sb[:, b, :].unsqueeze(1).unsqueeze(3).to_broadcast([P, width // 4, 4, 4]), ALU.mult)
-            elif mode != "AA":
-                nc.vector.tensor_copy(dst, h_rows[:].rearrange("p t (c i) -> p c t i", i=4))
-            else:
-                nc.scalar.copy(dst, h_rows[:].rearrange("p t (c i) -> p c t i", i=4))
+            nc.vector.tensor_tensor(
+                h_bf[:].rearrange("p (c i t) -> p c t i", i=2, t=4),
+                sig[:, :, c0 : c0 + width].rearrange("p t (c i) -> p c t i", i=2),
+                consts_ps[:, :, b].unsqueeze(1).unsqueeze(3).to_broadcast([P, width // 2, 4, 2]), ALU.mult)
+            return h_bf
+
+        def gain_on_scalar(sig, b, c0, width):
+            h_rows = ring.tile([P, 4, width], BF16, name="h_rows")
+            for t in range(4):
+                nc.scalar.activation(h_rows[:, t, :], sig[:, t, c0 : c0 + width], ACT.Copy,
+                                     scale=consts[:, t, b : b + 1])
+            h_bf = ring.tile([P, 4 * width], BF16, name="h_bf", align_bytes=64)
+            nc.scalar.copy(h_bf[:].rearrange("p (c i t) -> p c t i", i=4, t=4),
+                           h_rows[:].rearrange("p t (c i) -> p c t i", i=4))
+            return h_bf
+
+        def quantise(h_bf, j0, b):
+            width = h_bf.shape[1] // 4
             h_codes = held([P, width], U32, "h_codes_%d_%d" % (j0, b))
             h_sc = held([P, width], U8, "h_sc_%d_%d" % (j0, b))
             nc.vector.quantize_mx(out=h_codes[:].bitcast(FP8X4), scales=h_sc[:], in_=h_bf[:])
             return h_codes, h_sc
 
-        def stage2(j0, width, hq):
-            half, c0 = divmod(j0, HALF)
+        out_v = out.rearrange("(n p) j -> p n j", p=P)
+
+        def second_product(j0, width, hq, ahead, on_vector):
             step = HALF if width == HALF else P
-            per_bank = min(BANK // width, 3)
-            accs = [psum.tile([P, per_bank, width], F32, name="acc") for n0 in range(0, NT, per_bank)]
+            per_bank = HALF // width
+            accs = [psum.tile([P, per_bank, width], F32, name="acc") for n0 in range(0, 2 * PAIRS, per_bank)]
 
             def passes(bank, b):
                 h_codes, h_sc = hq[b]
-                spots = [(n, m0) for n in range(per_bank) for m0 in range(0, width, step)]
+                spots = [(u, m0) for u in range(per_bank) for m0 in range(0, width, step)]
                 for i, (u, m0) in enumerate(spots):
                     n = bank * per_bank + u
                     nc.tensor.matmul_mx(
@@ -216,28 +209,43 @@ def tile_list_measles_interchange_tracing_kernel(
                         rhs=h_codes[:, m0 : m0 + step].bitcast(FP8X4), rhs_scale=h_sc[:, m0 : m0 + step],
                         start=(b == 0 and i == 0), stop=(b == 1 and i == len(spots) - 1))
 
-            ahead = min(4, len(accs))
             for bank in range(ahead):
                 passes(bank, 0)
             cols = slice(j0, j0 + width)
-            prods = [res.tile([P, 2, width], F32, name="prod") for g in range(NT // 2)]
-            for bank, n0 in enumerate(range(0, NT, per_bank)):
+            prods = [ring.tile([P, 2, width], F32, name="prod") for g in range(PAIRS)]
+            scores = [res.tile([P, 2, width], F32, name="score") for g in range(PAIRS)]
+            later = []
+            for bank in range(len(accs)):
                 if bank >= ahead:
                     passes(bank, 0)
                 passes(bank, 1)
-                g, u = divmod(n0, 2)
+                g, u = divmod(bank * per_bank, 2)
                 rows = slice(u, u + per_bank)
                 nc.vector.tensor_tensor(prods[g][:, rows], accs[bank][:], given[0, g][:, rows, cols], ALU.mult)
-            for g in range(NT // 2):
-                score = res.tile([P, 2, width], F32, name="score")
-                engine = nc.gpsimd if g < GP_UNITS else nc.vector
-                engine.tensor_tensor(score[:], given[1, g][:, :, cols], prods[g][:], ALU.subtract)
+                if bank < len(accs) - on_vector:
+                    subtract(nc.gpsimd, scores[g], prods[g], g, rows, cols)
+                else:
+                    later.append((g, rows))
+            for g, rows in later:
+                subtract(nc.vector, scores[g], prods[g], g, rows, cols)
+
+        def subtract(engine, score, prod, g, rows, cols):
+            engine.tensor_tensor(score[:, rows], given[1, g][:, rows, cols], prod[:, rows], ALU.subtract)
+            if rows.stop == 2:
                 nc.sync.dma_start(out_v[:, 2 * g : 2 * g + 2, cols], score[:])
 
-        pending = None
-        for j0, width, mode0, mode1 in CHUNKS:
-            hq = [stage1(j0, width, 0, mode0), stage1(j0, width, 1, mode1)]
-            if pending is not None:
-                stage2(*pending)
-            pending = (j0, width, hq)
-        stage2(*pending)
+        sig00 = first_product(0, 0, placed([P, 4, HALF], F32, "sig00", W1_RAW_AT + 32 * QUART))
+        sig01 = first_product(0, 1)
+        hq0 = [quantise(gain_on_vector(sig00, 0, 0, HALF), 0, 0)]
+        sig10 = first_product(1, 0)
+        hq0.append(quantise(gain_on_vector(sig01, 1, 0, HALF), 0, 1))
+        sig11 = first_product(1, 1)
+        second_product(0, HALF, hq0, 3, 0)
+        h10 = gain_on_scalar(sig10, 0, 0, QUART)
+        h11 = gain_on_scalar(sig11, 1, 0, QUART)
+        h20 = gain_on_scalar(sig10, 0, QUART, QUART)
+        h21 = gain_on_vector(sig11, 1, QUART, QUART)
+        hq1 = [quantise(h10, HALF, 0), quantise(h11, HALF, 1)]
+        second_product(HALF, QUART, hq1, 0, 0)
+        hq2 = [quantise(h20, HALF + QUART, 0), quantise(h21, HALF + QUART, 1)]
+        second_product(HALF + QUART, QUART, hq2, 0, 3)

@@ -141,7 +141,8 @@ def tile_list_measles_interchange_tracing_kernel(
 
         prepare_weights(0)
         gather(v_sc, table_sc, 0, 1, placed([P, HALF], U8, "sc1_0", W1_RAW_AT))
-        deal(w_sc[1][:], w2_sc_raw[:])
+        nc.vector.tensor_copy(w_sc[1][:].rearrange("p (b t m) -> p b t m", t=4, m=P),
+                              w2_sc_raw[:].rearrange("p (b m t) -> p b t m", t=4, m=P))
         gather(v_sc, table_sc, 1, 1, placed([P, HALF], U8, "sc1_1", W2_SC_AT))
         gather(v_words, table, 0, 1, placed([P, HALF], U16, "words1_0", W2_SC_AT + HALF))
         prepare_weights(1)
@@ -221,7 +222,7 @@ def tile_list_measles_interchange_tracing_kernel(
                 passes(bank, 1)
                 g, u = divmod(bank * per_bank, 2)
                 rows = slice(u, u + per_bank)
-                nc.vector.tensor_tensor(prods[g][:, rows], accs[bank][:], given[0, g][:, rows, cols], ALU.mult)
+                nc.vector.tensor_tensor(prods[g][:, rows], given[0, g][:, rows, cols], accs[bank][:], ALU.mult)
                 if bank < len(accs) - on_vector:
                     subtract(nc.gpsimd, scores[g], prods[g], g, rows, cols)
                 else:
@@ -236,11 +237,12 @@ def tile_list_measles_interchange_tracing_kernel(
 
         sig00 = first_product(0, 0, placed([P, 4, HALF], F32, "sig00", W1_RAW_AT + 32 * QUART))
         sig01 = first_product(0, 1)
-        hq0 = [quantise(gain_on_vector(sig00, 0, 0, HALF), 0, 0)]
+        h00 = gain_on_vector(sig00, 0, 0, HALF)
         sig10 = first_product(1, 0)
-        hq0.append(quantise(gain_on_vector(sig01, 1, 0, HALF), 0, 1))
+        h01 = gain_on_vector(sig01, 1, 0, HALF)
+        hq0 = [quantise(h00, 0, 0), quantise(h01, 0, 1)]
         sig11 = first_product(1, 1)
-        second_product(0, HALF, hq0, 3, 0)
+        second_product(0, HALF, hq0, 1, 0)
         h10 = gain_on_scalar(sig10, 0, 0, QUART)
         h11 = gain_on_scalar(sig11, 1, 0, QUART)
         h20 = gain_on_scalar(sig10, 0, QUART, QUART)

@@ -20,7 +20,8 @@ ALU = mybir.AluOpType
 P = 128
 HALF = 512
 QUART = 256
-PAIRS = N // (2 * P)
+NT = N // P
+SCALAR_SHARE = 128
 W1_RAW_AT = 0
 W2_SC_AT = 4 * 16 * QUART
 W1_BF_AT = W2_SC_AT + H
@@ -99,10 +100,11 @@ def tile_list_measles_interchange_tracing_kernel(
         w3_codes = held([P, 2, 2 * N], U8, "w3_codes")
         nc.sync.dma_start(w3_codes[:].bitcast(I32), w3_words.rearrange("a p c -> p a c").bitcast(I32))
         given = {}
-        for x, g in ((0, 0), (0, 1), (0, 2), (1, 0), (1, 1), (1, 2)):
-            given[x, g] = held([P, 2, S], F32, "given%d%d" % (x, g))
-            rows = (hours, sus)[x].rearrange("(n p) j -> p n j", p=P)
-            nc.sync.dma_start(given[x, g][:], rows[:, 2 * g : 2 * g + 2, :])
+        for half in range(2):
+            for x in range(2):
+                given[x, half] = held([P, NT, HALF], F32, "given%d%d" % (x, half))
+                rows = (hours, sus)[x].rearrange("(n p) j -> p n j", p=P)
+                nc.sync.dma_start(given[x, half][:], rows[:, :, half * HALF : (half + 1) * HALF])
 
         consts_ps = psum_consts.tile([P, 4, P], F32, name="consts_ps")
         for t in range(4):
@@ -126,8 +128,8 @@ def tile_list_measles_interchange_tracing_kernel(
         w_sc = [held([P, H], U8, "w%d_sc" % k) for k in (1, 2)]
 
         def deal(dst, src):
-            nc.vector.tensor_copy(dst.rearrange("p (b t m) -> p b m t", t=4, m=P),
-                                  src.rearrange("p (b m t) -> p b m t", t=4, m=P))
+            nc.gpsimd.tensor_copy(dst.rearrange("p (b t m) -> p b t m", t=4, m=P),
+                                  src.rearrange("p (b m t) -> p b t m", t=4, m=P))
 
         def prepare_weights(b):
             cols = slice(b * HALF, (b + 1) * HALF)
@@ -141,8 +143,7 @@ def tile_list_measles_interchange_tracing_kernel(
 
         prepare_weights(0)
         gather(v_sc, table_sc, 0, 1, placed([P, HALF], U8, "sc1_0", W1_RAW_AT))
-        nc.vector.tensor_copy(w_sc[1][:].rearrange("p (b t m) -> p b t m", t=4, m=P),
-                              w2_sc_raw[:].rearrange("p (b m t) -> p b t m", t=4, m=P))
+        deal(w_sc[1][:], w2_sc_raw[:])
         gather(v_sc, table_sc, 1, 1, placed([P, HALF], U8, "sc1_1", W2_SC_AT))
         gather(v_words, table, 0, 1, placed([P, HALF], U16, "words1_0", W2_SC_AT + HALF))
         prepare_weights(1)
@@ -166,88 +167,96 @@ def tile_list_measles_interchange_tracing_kernel(
                 nc.scalar.activation(sig[:, t, :], accs[t][:], ACT.Sigmoid, bias=consts[:, t, 2 + b : 3 + b])
             return sig
 
-        def gain_on_vector(sig, b, c0, width):
-            h_bf = ring.tile([P, 4 * width], BF16, name="h_bf", align_bytes=64)
+        def gain_on_vector(dst, sig, b, c0, c1):
             nc.vector.tensor_tensor(
-                h_bf[:].rearrange("p (c i t) -> p c t i", i=2, t=4),
-                sig[:, :, c0 : c0 + width].rearrange("p t (c i) -> p c t i", i=2),
-                consts_ps[:, :, b].unsqueeze(1).unsqueeze(3).to_broadcast([P, width // 2, 4, 2]), ALU.mult)
-            return h_bf
+                dst.rearrange("p (c i t) -> p c t i", i=2, t=4),
+                sig[:, :, c0:c1].rearrange("p t (c i) -> p c t i", i=2),
+                consts_ps[:, :, b].unsqueeze(1).unsqueeze(3).to_broadcast([P, (c1 - c0) // 2, 4, 2]), ALU.mult)
 
-        def gain_on_scalar(sig, b, c0, width):
-            h_rows = ring.tile([P, 4, width], BF16, name="h_rows")
+        def gain_on_scalar(dst, sig, b, c0, c1):
+            h_rows = ring.tile([P, 4, c1 - c0], BF16, name="h_rows")
             for t in range(4):
-                nc.scalar.activation(h_rows[:, t, :], sig[:, t, c0 : c0 + width], ACT.Copy,
-                                     scale=consts[:, t, b : b + 1])
-            h_bf = ring.tile([P, 4 * width], BF16, name="h_bf", align_bytes=64)
-            nc.scalar.copy(h_bf[:].rearrange("p (c i t) -> p c t i", i=4, t=4),
+                nc.scalar.activation(h_rows[:, t, :], sig[:, t, c0:c1], ACT.Copy, scale=consts[:, t, b : b + 1])
+            nc.scalar.copy(dst.rearrange("p (c i t) -> p c t i", i=4, t=4),
                            h_rows[:].rearrange("p t (c i) -> p c t i", i=4))
-            return h_bf
 
-        def quantise(h_bf, j0, b):
-            width = h_bf.shape[1] // 4
-            h_codes = held([P, width], U32, "h_codes_%d_%d" % (j0, b))
-            h_sc = held([P, width], U8, "h_sc_%d_%d" % (j0, b))
-            nc.vector.quantize_mx(out=h_codes[:].bitcast(FP8X4), scales=h_sc[:], in_=h_bf[:])
-            return h_codes, h_sc
+        h_bf = [held([P, 4 * HALF], BF16, "h_bf%d" % i) for i in range(4)]
+        h_codes = [held([P, HALF], U32, "h_codes%d" % i) for i in range(4)]
+        h_sc = [held([P, HALF], U8, "h_sc%d" % i) for i in range(4)]
+
+        def quantise(i):
+            nc.vector.quantize_mx(out=h_codes[i][:].bitcast(FP8X4), scales=h_sc[i][:], in_=h_bf[i][:])
 
         out_v = out.rearrange("(n p) j -> p n j", p=P)
+        scores = [held([P, NT, HALF], F32, "score%d" % half) for half in range(2)]
 
-        def second_product(j0, width, hq, ahead, on_vector):
-            step = HALF if width == HALF else P
-            per_bank = HALF // width
-            accs = [psum.tile([P, per_bank, width], F32, name="acc") for n0 in range(0, 2 * PAIRS, per_bank)]
+        def one_pass(acc, n, b, i, c0, width, start, stop):
+            nc.tensor.matmul_mx(
+                out=acc, lhsT=w3_codes[:, b, 2 * P * n : 2 * P * (n + 1)].bitcast(FP4X4),
+                lhsT_scale=w3_sc[:, b, P * n : P * (n + 1)],
+                rhs=h_codes[i][:, c0 : c0 + width].bitcast(FP8X4), rhs_scale=h_sc[i][:, c0 : c0 + width],
+                start=start, stop=stop)
 
-            def passes(bank, b):
-                h_codes, h_sc = hq[b]
-                spots = [(u, m0) for u in range(per_bank) for m0 in range(0, width, step)]
-                for i, (u, m0) in enumerate(spots):
-                    n = bank * per_bank + u
-                    nc.tensor.matmul_mx(
-                        out=accs[bank][:, u, m0 : m0 + step],
-                        lhsT=w3_codes[:, b, 2 * P * n : 2 * P * (n + 1)].bitcast(FP4X4),
-                        lhsT_scale=w3_sc[:, b, P * n : P * (n + 1)],
-                        rhs=h_codes[:, m0 : m0 + step].bitcast(FP8X4), rhs_scale=h_sc[:, m0 : m0 + step],
-                        start=(b == 0 and i == 0), stop=(b == 1 and i == len(spots) - 1))
+        def weigh(acc, half, rows, cols):
+            prod = res.tile([P, HALF], F32, name="prod")
+            shaped = prod[:].rearrange("p (n j) -> p n j", n=rows.stop - rows.start)
+            nc.vector.tensor_tensor(shaped, given[0, half][:, rows, cols], acc, ALU.mult)
+            return shaped, half, rows, cols
 
-            for bank in range(ahead):
-                passes(bank, 0)
-            cols = slice(j0, j0 + width)
-            prods = [ring.tile([P, 2, width], F32, name="prod") for g in range(PAIRS)]
-            scores = [res.tile([P, 2, width], F32, name="score") for g in range(PAIRS)]
-            later = []
-            for bank in range(len(accs)):
-                if bank >= ahead:
-                    passes(bank, 0)
-                passes(bank, 1)
-                g, u = divmod(bank * per_bank, 2)
-                rows = slice(u, u + per_bank)
-                nc.vector.tensor_tensor(prods[g][:, rows], given[0, g][:, rows, cols], accs[bank][:], ALU.mult)
-                if bank < len(accs) - on_vector:
-                    subtract(nc.gpsimd, scores[g], prods[g], g, rows, cols)
+        def subtract(engine, prod, half, rows, cols):
+            engine.tensor_tensor(scores[half][:, rows, cols], given[1, half][:, rows, cols], prod, ALU.subtract)
+            if cols.stop == HALF:
+                nc.sync.dma_start(out_v[:, rows, half * HALF : (half + 1) * HALF], scores[half][:, rows, :])
+
+        def second_product_quarter(c, on_gpsimd):
+            left = []
+            for g in range(NT // 2):
+                acc = psum.tile([P, 2, QUART], F32, name="acc")
+                spots = [(b, u, m0) for b in range(2) for u in range(2) for m0 in range(0, QUART, P)]
+                for i, (b, u, m0) in enumerate(spots):
+                    one_pass(acc[:, u, m0 : m0 + P], 2 * g + u, b, c, b * QUART + m0, P, i == 0, i == len(spots) - 1)
+                weighed = weigh(acc[:], 0, slice(2 * g, 2 * g + 2), slice(c * QUART, (c + 1) * QUART))
+                if g < on_gpsimd:
+                    subtract(nc.gpsimd, *weighed)
                 else:
-                    later.append((g, rows))
-            for g, rows in later:
-                subtract(nc.vector, scores[g], prods[g], g, rows, cols)
+                    left.append(weighed)
+            return left
 
-        def subtract(engine, score, prod, g, rows, cols):
-            engine.tensor_tensor(score[:, rows], given[1, g][:, rows, cols], prod[:, rows], ALU.subtract)
-            if rows.stop == 2:
-                nc.sync.dma_start(out_v[:, 2 * g : 2 * g + 2, cols], score[:])
+        def second_product_half(ahead, on_gpsimd):
+            accs = [psum.tile([P, 1, HALF], F32, name="acc") for n in range(NT)]
+            for n in range(ahead):
+                one_pass(accs[n][:, 0], n, 1, 3, 0, HALF, True, False)
+            left = []
+            for n in range(NT):
+                if n >= ahead:
+                    one_pass(accs[n][:, 0], n, 1, 3, 0, HALF, True, False)
+                one_pass(accs[n][:, 0], n, 0, 2, 0, HALF, False, True)
+                weighed = weigh(accs[n][:], 1, slice(n, n + 1), slice(0, HALF))
+                if n < on_gpsimd:
+                    subtract(nc.gpsimd, *weighed)
+                else:
+                    left.append(weighed)
+            return left
+
+        def first_half_gain(c, b, sig):
+            gain_on_vector(h_bf[c][:, 4 * QUART * b : 4 * QUART * (b + 1)], sig, b, c * QUART, (c + 1) * QUART)
 
         sig00 = first_product(0, 0, placed([P, 4, HALF], F32, "sig00", W1_RAW_AT + 32 * QUART))
         sig01 = first_product(0, 1)
-        h00 = gain_on_vector(sig00, 0, 0, HALF)
+        first_half_gain(0, 0, sig00)
+        first_half_gain(1, 0, sig00)
         sig10 = first_product(1, 0)
-        h01 = gain_on_vector(sig01, 1, 0, HALF)
-        hq0 = [quantise(h00, 0, 0), quantise(h01, 0, 1)]
+        first_half_gain(0, 1, sig01)
+        quantise(0)
+        first_half_gain(1, 1, sig01)
         sig11 = first_product(1, 1)
-        second_product(0, HALF, hq0, 1, 0)
-        h10 = gain_on_scalar(sig10, 0, 0, QUART)
-        h11 = gain_on_scalar(sig11, 1, 0, QUART)
-        h20 = gain_on_scalar(sig10, 0, QUART, QUART)
-        h21 = gain_on_vector(sig11, 1, QUART, QUART)
-        hq1 = [quantise(h10, HALF, 0), quantise(h11, HALF, 1)]
-        second_product(HALF, QUART, hq1, 0, 0)
-        hq2 = [quantise(h20, HALF + QUART, 0), quantise(h21, HALF + QUART, 1)]
-        second_product(HALF + QUART, QUART, hq2, 0, 3)
+        second_product_quarter(0, 3)
+        quantise(1)
+        gain_on_scalar(h_bf[3][:, 0 : 4 * SCALAR_SHARE], sig11, 1, 0, SCALAR_SHARE)
+        gain_on_scalar(h_bf[2][:], sig10, 0, 0, HALF)
+        gain_on_vector(h_bf[3][:, 4 * SCALAR_SHARE : 4 * HALF], sig11, 1, SCALAR_SHARE, HALF)
+        quantise(3)
+        second_product_quarter(1, 3)
+        quantise(2)
+        for weighed in second_product_half(4, 1):
+            subtract(nc.vector, *weighed)

@@ -128,8 +128,8 @@ def tile_list_measles_interchange_tracing_kernel(
         w_sc = [held([P, H], U8, "w%d_sc" % k) for k in (1, 2)]
 
         def deal(dst, src):
-            nc.gpsimd.tensor_copy(dst.rearrange("p (b t m) -> p b t m", t=4, m=P),
-                                  src.rearrange("p (b m t) -> p b t m", t=4, m=P))
+            nc.vector.tensor_copy(dst.rearrange("p (b t m) -> p b m t", t=4, m=P),
+                                  src.rearrange("p (b m t) -> p b m t", t=4, m=P))
 
         def prepare_weights(b):
             cols = slice(b * HALF, (b + 1) * HALF)

@@ -21,10 +21,11 @@ P = 128
 HALF = 512
 QUART = 256
 NT = N // P
-SCALAR_SHARE = 128
+SCALAR_SHARE = 192
 W1_RAW_AT = 0
 W2_SC_AT = 4 * 16 * QUART
 W1_BF_AT = W2_SC_AT + H
+LAST_BF_AT = W1_BF_AT + 16 * HALF
 
 
 def tile_list_measles_interchange_tracing_kernel(
@@ -39,7 +40,8 @@ def tile_list_measles_interchange_tracing_kernel(
         shared = ctx.enter_context(tc.tile_pool(name="shared", bufs=1))
         res = ctx.enter_context(tc.tile_pool(name="res", bufs=6))
         psum_consts = ctx.enter_context(tc.psum_pool(name="psum_consts", bufs=1))
-        psum = ctx.enter_context(tc.psum_pool(name="psum", bufs=7))
+        psum_four = ctx.enter_context(tc.psum_pool(name="psum_four", bufs=4))
+        psum_three = ctx.enter_context(tc.psum_pool(name="psum_three", bufs=3))
 
         def held(shape, dtype, name, tag=None):
             return keep.tile(shape, dtype, name=name, tag=tag or name, align_bytes=64)
@@ -152,7 +154,7 @@ def tile_list_measles_interchange_tracing_kernel(
         def first_product(half, b, sig=None):
             if sig is None:
                 sig = ring.tile([P, 4, HALF], F32, name="sig")
-            accs = [psum.tile([P, HALF], F32, name="acc") for t in range(4)]
+            accs = [psum_four.tile([P, HALF], F32, name="acc") for t in range(4)]
 
             def one_pass(t, k, first):
                 wc = slice(b * HALF + t * P, b * HALF + (t + 1) * P)
@@ -160,10 +162,14 @@ def tile_list_measles_interchange_tracing_kernel(
                     out=accs[t][:], lhsT=w_codes[k][:, wc].bitcast(FP8X4), lhsT_scale=w_sc[k][:, wc],
                     rhs=v_words[k, half].bitcast(FP4X4), rhs_scale=v_sc[k, half], start=first, stop=not first)
 
+            first_unit = half == 0 and b == 0
+            if first_unit:
+                for t in range(4):
+                    one_pass(t, 0, True)
             for t in range(4):
-                one_pass(t, b, True)
-            for t in range(4):
-                one_pass(t, 1 - b, False)
+                if not first_unit:
+                    one_pass(t, 0, True)
+                one_pass(t, 1, False)
                 nc.scalar.activation(sig[:, t, :], accs[t][:], ACT.Sigmoid, bias=consts[:, t, 2 + b : 3 + b])
             return sig
 
@@ -173,14 +179,24 @@ def tile_list_measles_interchange_tracing_kernel(
                 sig[:, :, c0:c1].rearrange("p t (c i) -> p c t i", i=2),
                 consts_ps[:, :, b].unsqueeze(1).unsqueeze(3).to_broadcast([P, (c1 - c0) // 2, 4, 2]), ALU.mult)
 
+        def interleave_on_scalar(dst, h_rows):
+            nc.scalar.copy(dst.rearrange("p (c i t) -> p c t i", i=4, t=4),
+                           h_rows[:].rearrange("p t (c i) -> p c t i", i=4))
+
         def gain_on_scalar(dst, sig, b, c0, c1):
             h_rows = ring.tile([P, 4, c1 - c0], BF16, name="h_rows")
             for t in range(4):
                 nc.scalar.activation(h_rows[:, t, :], sig[:, t, c0:c1], ACT.Copy, scale=consts[:, t, b : b + 1])
-            nc.scalar.copy(dst.rearrange("p (c i t) -> p c t i", i=4, t=4),
-                           h_rows[:].rearrange("p t (c i) -> p c t i", i=4))
+            interleave_on_scalar(dst, h_rows)
 
-        h_bf = [held([P, 4 * HALF], BF16, "h_bf%d" % i) for i in range(4)]
+        def gain_on_gpsimd(sig, b):
+            h_rows = ring.tile([P, 4, HALF], BF16, name="h_rows")
+            for t in range(4):
+                nc.gpsimd.tensor_scalar(h_rows[:, t, :], sig[:, t, :], consts[:, t, b : b + 1], 0.0, ALU.mult, ALU.add)
+            return h_rows
+
+        h_bf = [held([P, 4 * HALF], BF16, "h_bf%d" % i) for i in (0, 1, 3)]
+        h_bf.insert(2, placed([P, 4 * HALF], BF16, "h_bf2", LAST_BF_AT))
         h_codes = [held([P, HALF], U32, "h_codes%d" % i) for i in range(4)]
         h_sc = [held([P, HALF], U8, "h_sc%d" % i) for i in range(4)]
 
@@ -197,25 +213,28 @@ def tile_list_measles_interchange_tracing_kernel(
                 rhs=h_codes[i][:, c0 : c0 + width].bitcast(FP8X4), rhs_scale=h_sc[i][:, c0 : c0 + width],
                 start=start, stop=stop)
 
-        def weigh(acc, half, rows, cols):
-            prod = res.tile([P, HALF], F32, name="prod")
-            shaped = prod[:].rearrange("p (n j) -> p n j", n=rows.stop - rows.start)
+        def weigh(acc, half, rows, cols, prod=None):
+            if prod is None:
+                prod = res.tile([P, HALF], F32, name="prod")[:, :]
+            shaped = prod.rearrange("p (n j) -> p n j", n=rows.stop - rows.start)
             nc.vector.tensor_tensor(shaped, given[0, half][:, rows, cols], acc, ALU.mult)
             return shaped, half, rows, cols
 
         def subtract(engine, prod, half, rows, cols):
             engine.tensor_tensor(scores[half][:, rows, cols], given[1, half][:, rows, cols], prod, ALU.subtract)
-            if cols.stop == HALF:
-                nc.sync.dma_start(out_v[:, rows, half * HALF : (half + 1) * HALF], scores[half][:, rows, :])
+            queue = nc.scalar if engine is nc.vector and half == 1 else nc.sync
+            queue.dma_start(out_v[:, rows, half * HALF + cols.start : half * HALF + cols.stop],
+                            scores[half][:, rows, cols])
 
-        def second_product_quarter(c, on_gpsimd):
+        def second_product_quarter(c, on_gpsimd, prods=None):
             left = []
             for g in range(NT // 2):
-                acc = psum.tile([P, 2, QUART], F32, name="acc")
+                acc = psum_three.tile([P, 2, QUART], F32, name="acc")
                 spots = [(b, u, m0) for b in range(2) for u in range(2) for m0 in range(0, QUART, P)]
                 for i, (b, u, m0) in enumerate(spots):
                     one_pass(acc[:, u, m0 : m0 + P], 2 * g + u, b, c, b * QUART + m0, P, i == 0, i == len(spots) - 1)
-                weighed = weigh(acc[:], 0, slice(2 * g, 2 * g + 2), slice(c * QUART, (c + 1) * QUART))
+                weighed = weigh(acc[:], 0, slice(2 * g, 2 * g + 2), slice(c * QUART, (c + 1) * QUART),
+                                None if prods is None else prods[:, g])
                 if g < on_gpsimd:
                     subtract(nc.gpsimd, *weighed)
                 else:
@@ -223,7 +242,7 @@ def tile_list_measles_interchange_tracing_kernel(
             return left
 
         def second_product_half(ahead, on_gpsimd):
-            accs = [psum.tile([P, 1, HALF], F32, name="acc") for n in range(NT)]
+            accs = [(psum_four if n < 4 else psum_three).tile([P, 1, HALF], F32, name="acc") for n in range(NT)]
             for n in range(ahead):
                 one_pass(accs[n][:, 0], n, 1, 3, 0, HALF, True, False)
             left = []
@@ -246,17 +265,20 @@ def tile_list_measles_interchange_tracing_kernel(
         first_half_gain(0, 0, sig00)
         first_half_gain(1, 0, sig00)
         sig10 = first_product(1, 0)
+        rows10 = gain_on_gpsimd(sig10, 0)
         first_half_gain(0, 1, sig01)
         quantise(0)
         first_half_gain(1, 1, sig01)
-        sig11 = first_product(1, 1)
-        second_product_quarter(0, 3)
         quantise(1)
+        sig11 = first_product(1, 1)
+        left = second_product_quarter(0, 2)
         gain_on_scalar(h_bf[3][:, 0 : 4 * SCALAR_SHARE], sig11, 1, 0, SCALAR_SHARE)
-        gain_on_scalar(h_bf[2][:], sig10, 0, 0, HALF)
+        interleave_on_scalar(h_bf[2][:], rows10)
         gain_on_vector(h_bf[3][:, 4 * SCALAR_SHARE : 4 * HALF], sig11, 1, SCALAR_SHARE, HALF)
+        for weighed in left:
+            subtract(nc.vector, *weighed)
         quantise(3)
-        second_product_quarter(1, 3)
         quantise(2)
-        for weighed in second_product_half(4, 1):
+        second_product_quarter(1, 3, placed([P, NT // 2, HALF], F32, "late_prods", LAST_BF_AT))
+        for weighed in second_product_half(4, 0):
             subtract(nc.vector, *weighed)

@@ -21,7 +21,7 @@ P = 128
 HALF = 512
 QUART = 256
 NT = N // P
-SCALAR_SHARE = 192
+SCALAR_SHARE = 128
 W1_RAW_AT = 0
 W2_SC_AT = 4 * 16 * QUART
 W1_BF_AT = W2_SC_AT + H
@@ -108,11 +108,11 @@ def tile_list_measles_interchange_tracing_kernel(
                 rows = (hours, sus)[x].rearrange("(n p) j -> p n j", p=P)
                 nc.sync.dma_start(given[x, half][:], rows[:, :, half * HALF : (half + 1) * HALF])
 
-        consts_ps = psum_consts.tile([P, 4, P], F32, name="consts_ps")
+        consts_ps = psum_consts.tile([P, P, 4], F32, name="consts_ps")
         for t in range(4):
-            nc.tensor.transpose(consts_ps[:, t, :], const_rows[:, t:HALF:4], identity[:])
+            nc.tensor.transpose(consts_ps[:, :, t], const_rows[:, t:HALF:4], identity[:])
         consts = held([P, 4, 4], F32, "consts")
-        nc.scalar.copy(consts[:], consts_ps[:, :, 0:4])
+        nc.scalar.copy(consts[:], consts_ps[:, 0:4, :])
 
         v_words, v_sc = {}, {}
 
@@ -170,14 +170,14 @@ def tile_list_measles_interchange_tracing_kernel(
                 if not first_unit:
                     one_pass(t, 0, True)
                 one_pass(t, 1, False)
-                nc.scalar.activation(sig[:, t, :], accs[t][:], ACT.Sigmoid, bias=consts[:, t, 2 + b : 3 + b])
+                nc.scalar.activation(sig[:, t, :], accs[t][:], ACT.Sigmoid, bias=consts[:, 2 + b, t : t + 1])
             return sig
 
         def gain_on_vector(dst, sig, b, c0, c1):
             nc.vector.tensor_tensor(
                 dst.rearrange("p (c i t) -> p c t i", i=2, t=4),
                 sig[:, :, c0:c1].rearrange("p t (c i) -> p c t i", i=2),
-                consts_ps[:, :, b].unsqueeze(1).unsqueeze(3).to_broadcast([P, (c1 - c0) // 2, 4, 2]), ALU.mult)
+                consts_ps[:, b, :].unsqueeze(1).unsqueeze(3).to_broadcast([P, (c1 - c0) // 2, 4, 2]), ALU.mult)
 
         def interleave_on_scalar(dst, h_rows):
             nc.scalar.copy(dst.rearrange("p (c i t) -> p c t i", i=4, t=4),
@@ -186,14 +186,8 @@ def tile_list_measles_interchange_tracing_kernel(
         def gain_on_scalar(dst, sig, b, c0, c1):
             h_rows = ring.tile([P, 4, c1 - c0], BF16, name="h_rows")
             for t in range(4):
-                nc.scalar.activation(h_rows[:, t, :], sig[:, t, c0:c1], ACT.Copy, scale=consts[:, t, b : b + 1])
+                nc.scalar.activation(h_rows[:, t, :], sig[:, t, c0:c1], ACT.Copy, scale=consts[:, b, t : t + 1])
             interleave_on_scalar(dst, h_rows)
-
-        def gain_on_gpsimd(sig, b):
-            h_rows = ring.tile([P, 4, HALF], BF16, name="h_rows")
-            for t in range(4):
-                nc.gpsimd.tensor_scalar(h_rows[:, t, :], sig[:, t, :], consts[:, t, b : b + 1], 0.0, ALU.mult, ALU.add)
-            return h_rows
 
         h_bf = [held([P, 4 * HALF], BF16, "h_bf%d" % i) for i in (0, 1, 3)]
         h_bf.insert(2, placed([P, 4 * HALF], BF16, "h_bf2", LAST_BF_AT))
@@ -204,7 +198,7 @@ def tile_list_measles_interchange_tracing_kernel(
             nc.vector.quantize_mx(out=h_codes[i][:].bitcast(FP8X4), scales=h_sc[i][:], in_=h_bf[i][:])
 
         out_v = out.rearrange("(n p) j -> p n j", p=P)
-        scores = [held([P, NT, HALF], F32, "score%d" % half) for half in range(2)]
+        scores = {(0, 0): held([P, NT, QUART], F32, "scores_first"), (1, 0): held([P, NT, HALF], F32, "scores_last")}
 
         def one_pass(acc, n, b, i, c0, width, start, stop):
             nc.tensor.matmul_mx(
@@ -213,28 +207,26 @@ def tile_list_measles_interchange_tracing_kernel(
                 rhs=h_codes[i][:, c0 : c0 + width].bitcast(FP8X4), rhs_scale=h_sc[i][:, c0 : c0 + width],
                 start=start, stop=stop)
 
-        def weigh(acc, half, rows, cols, prod=None):
-            if prod is None:
-                prod = res.tile([P, HALF], F32, name="prod")[:, :]
-            shaped = prod.rearrange("p (n j) -> p n j", n=rows.stop - rows.start)
+        def weigh(acc, half, rows, cols):
+            prod = res.tile([P, HALF], F32, name="prod", bufs=NT + NT // 2)
+            shaped = prod[:].rearrange("p (n j) -> p n j", n=rows.stop - rows.start)
             nc.vector.tensor_tensor(shaped, given[0, half][:, rows, cols], acc, ALU.mult)
             return shaped, half, rows, cols
 
         def subtract(engine, prod, half, rows, cols):
-            engine.tensor_tensor(scores[half][:, rows, cols], given[1, half][:, rows, cols], prod, ALU.subtract)
+            score = scores[half, cols.start][:, rows]
+            engine.tensor_tensor(score, given[1, half][:, rows, cols], prod, ALU.subtract)
             queue = nc.scalar if engine is nc.vector and half == 1 else nc.sync
-            queue.dma_start(out_v[:, rows, half * HALF + cols.start : half * HALF + cols.stop],
-                            scores[half][:, rows, cols])
+            queue.dma_start(out_v[:, rows, half * HALF + cols.start : half * HALF + cols.stop], score)
 
-        def second_product_quarter(c, on_gpsimd, prods=None):
+        def second_product_quarter(c, on_gpsimd):
             left = []
             for g in range(NT // 2):
                 acc = psum_three.tile([P, 2, QUART], F32, name="acc")
                 spots = [(b, u, m0) for b in range(2) for u in range(2) for m0 in range(0, QUART, P)]
                 for i, (b, u, m0) in enumerate(spots):
                     one_pass(acc[:, u, m0 : m0 + P], 2 * g + u, b, c, b * QUART + m0, P, i == 0, i == len(spots) - 1)
-                weighed = weigh(acc[:], 0, slice(2 * g, 2 * g + 2), slice(c * QUART, (c + 1) * QUART),
-                                None if prods is None else prods[:, g])
+                weighed = weigh(acc[:], 0, slice(2 * g, 2 * g + 2), slice(c * QUART, (c + 1) * QUART))
                 if g < on_gpsimd:
                     subtract(nc.gpsimd, *weighed)
                 else:
@@ -265,7 +257,6 @@ def tile_list_measles_interchange_tracing_kernel(
         first_half_gain(0, 0, sig00)
         first_half_gain(1, 0, sig00)
         sig10 = first_product(1, 0)
-        rows10 = gain_on_gpsimd(sig10, 0)
         first_half_gain(0, 1, sig01)
         quantise(0)
         first_half_gain(1, 1, sig01)
@@ -273,12 +264,15 @@ def tile_list_measles_interchange_tracing_kernel(
         sig11 = first_product(1, 1)
         left = second_product_quarter(0, 2)
         gain_on_scalar(h_bf[3][:, 0 : 4 * SCALAR_SHARE], sig11, 1, 0, SCALAR_SHARE)
-        interleave_on_scalar(h_bf[2][:], rows10)
+        gain_on_scalar(h_bf[2][:], sig10, 0, 0, HALF)
         gain_on_vector(h_bf[3][:, 4 * SCALAR_SHARE : 4 * HALF], sig11, 1, SCALAR_SHARE, HALF)
         for weighed in left:
             subtract(nc.vector, *weighed)
         quantise(3)
+        left = second_product_quarter(1, 0)
         quantise(2)
-        second_product_quarter(1, 3, placed([P, NT // 2, HALF], F32, "late_prods", LAST_BF_AT))
+        scores[0, QUART] = placed([P, NT, QUART], F32, "scores_second", LAST_BF_AT)
+        for weighed in left:
+            subtract(nc.gpsimd, *weighed)
         for weighed in second_product_half(4, 0):
             subtract(nc.vector, *weighed)

@@ -21,10 +21,10 @@ P = 128
 HALF = 512
 QUART = 256
 NT = N // P
+ROWS_AT = P - 16
 SCALAR_SHARE = 128
 W1_RAW_AT = 0
-W2_SC_AT = 4 * 16 * QUART
-W1_BF_AT = W2_SC_AT + H
+W1_BF_AT = 4 * 16 * QUART
 LAST_BF_AT = W1_BF_AT + 16 * HALF
 
 
@@ -49,6 +49,10 @@ def tile_list_measles_interchange_tracing_kernel(
         def placed(shape, dtype, name, offset):
             return shared.tile(shape, dtype, name=name, offset=offset, align_bytes=64)
 
+        warm = held([P, 16], F32, "warm")
+        nc.gpsimd.memset(warm[:, 0:1], 0.0)
+        nc.scalar.activation(warm[:, 8:9], warm[:, 0:1], ACT.Sigmoid)
+
         list_a = lists.tile([P, S // 16], U16, name="list_a")
         list_b = lists.tile([P, S // 16], U16, name="list_b")
         nc.sync.dma_start(list_a[:], offs)
@@ -61,21 +65,25 @@ def tile_list_measles_interchange_tracing_kernel(
 
         table = held([P, T], U16, "table")
         table_sc = held([P, T], U8, "table_sc")
-        nc.vector.memset(table_sc[:, 0 : T // 2].bitcast(I32), 0)
-        nc.gpsimd.memset(table_sc[:, T // 2 : T].bitcast(I32), 0)
-        load_scale_rows(table_sc, tab_scales[0])
-        nc.sync.dma_start(table[:].bitcast(I32), tab_words[0].bitcast(I32))
-
-        w2_sc_raw = placed([P, H], U8, "w2_sc_raw", W2_SC_AT)
+        nc.sync.dma_start(table_sc[ROWS_AT:P].bitcast(I32), tab_scales[0].bitcast(I32))
+        w2_sc_raw = held([P, H], U8, "w2_sc_raw")
         nc.vector.memset(w2_sc_raw[:].bitcast(I32), 0)
-        w3_sc = held([P, 2, N], U8, "w3_sc")
-        nc.vector.memset(w3_sc[:].rearrange("p a c -> p (a c)").bitcast(I32), 0)
         const_rows = held([P, HALF], F32, "const_rows")
         nc.gpsimd.memset(const_rows[:], 0.0)
+        nc.gpsimd.memset(table_sc[0:96].bitcast(I32), 0)
+        nc.vector.memset(table_sc[96:ROWS_AT].bitcast(I32), 0)
+        planes = [held([P, 2, HALF], U8, "plane%d" % half) for half in range(2)]
+        for plane in planes:
+            nc.vector.memset(plane[:].rearrange("p k c -> p (k c)").bitcast(I32), 0)
+        nc.sync.dma_start(table[:].bitcast(I32), tab_words[0].bitcast(I32))
+        nc.sync.dma_start(const_rows[0:2, :], gain.rearrange("(b c) -> b c", b=2))
+        nc.sync.dma_start(const_rows[2:4, :], bias.rearrange("(b c) -> b c", b=2))
+        load_scale_rows(w2_sc_raw, w2_scales[0])
+
+        w3_sc = held([P, 2, N], U8, "w3_sc")
+        nc.vector.memset(w3_sc[:].rearrange("p a c -> p (a c)").bitcast(I32), 0)
         identity = held([P, P], F32, "identity")
         make_identity(nc, identity[:])
-        warm_out = held([P, 8], F32, "warm_out")
-        nc.scalar.activation(warm_out[:, 0:1], identity[:, 0:1], ACT.Sigmoid)
 
         w1_rows = w1.rearrange("(p j) c -> p j c", j=4)
         w2_flat = w2_words[0].rearrange("p c i -> p (c i)").bitcast(I32)
@@ -91,22 +99,7 @@ def tile_list_measles_interchange_tracing_kernel(
 
         load_w1(0)
         load_w1(1)
-        nc.sync.dma_start(const_rows[0:2, :], gain.rearrange("(b c) -> b c", b=2))
-        nc.sync.dma_start(const_rows[2:4, :], bias.rearrange("(b c) -> b c", b=2))
         load_w2(0)
-        load_scale_rows(w2_sc_raw, w2_scales[0])
-        load_w1(2)
-        load_w1(3)
-        load_w2(1)
-        load_scale_rows(w3_sc, w3_scales.rearrange("a r c -> r a c"))
-        w3_codes = held([P, 2, 2 * N], U8, "w3_codes")
-        nc.sync.dma_start(w3_codes[:].bitcast(I32), w3_words.rearrange("a p c -> p a c").bitcast(I32))
-        given = {}
-        for half in range(2):
-            for x in range(2):
-                given[x, half] = held([P, NT, HALF], F32, "given%d%d" % (x, half))
-                rows = (hours, sus)[x].rearrange("(n p) j -> p n j", p=P)
-                nc.sync.dma_start(given[x, half][:], rows[:, :, half * HALF : (half + 1) * HALF])
 
         consts_ps = psum_consts.tile([P, P, 4], F32, name="consts_ps")
         for t in range(4):
@@ -121,12 +114,43 @@ def tile_list_measles_interchange_tracing_kernel(
             store[k, half] = dst[:]
             nc.vector.tensor_copy(dst[:], window[:].indirect(both[k][:, cols]))
 
-        for k in range(2):
-            gather(v_sc, table_sc, k, 0, held([P, HALF], U8, "sc0_%d" % k))
+        def gather_scales(half, picked):
+            cols = slice(half * HALF // 16, (half + 1) * HALF // 16)
+            for k in range(2):
+                nc.vector.tensor_copy(picked[:, k], table_sc[:].indirect(both[k][:, cols]))
+                v_sc[k, half] = planes[half][:, k]
+            return picked
+
+        def carry_scales(half, picked):
+            for r in range(4):
+                nc.sync.dma_start(planes[half][r:P:32].rearrange("p k c -> p (k c)").bitcast(I32),
+                                  picked[ROWS_AT + r : P : 4].rearrange("p k c -> p (k c)").bitcast(I32))
+
+        carry_scales(0, gather_scales(0, held([P, 2, HALF], U8, "picked0")))
+        load_w1(2)
+        load_w1(3)
+        load_w2(1)
+        load_scale_rows(w3_sc, w3_scales.rearrange("a r c -> r a c"))
+        w3_codes = held([P, 2, 2 * N], U8, "w3_codes")
+        nc.sync.dma_start(w3_codes[:].bitcast(I32), w3_words.rearrange("a p c -> p a c").bitcast(I32))
+        given = {}
+
+        def load_given(x, half, n0, n1):
+            tile = held([P, n1 - n0, HALF], F32, "given%d%d%d" % (x, half, n0))
+            rows = (hours, sus)[x].rearrange("(n p) j -> p n j", p=P)
+            nc.sync.dma_start(tile[:], rows[:, n0:n1, half * HALF : (half + 1) * HALF])
+            for n in range(n0, n1):
+                given[x, half, n] = tile, n - n0
+
+        def given_rows(x, half, rows, cols):
+            tile, first = given[x, half, rows.start]
+            return tile[:, first : first + rows.stop - rows.start, cols]
+
+        load_given(0, 0, 0, 2)
         for k in range(2):
             gather(v_words, table, k, 0, held([P, HALF], U16, "words0_%d" % k))
 
-        w_codes = [held([P, H], U32, "w%d_codes" % k) for k in (1, 2)]
+        w_codes = {(k, b): held([P, HALF], U32, "w%d_codes%d" % (k, b)) for k in range(2) for b in range(2)}
         w_sc = [held([P, H], U8, "w%d_sc" % k) for k in (1, 2)]
 
         def deal(dst, src):
@@ -140,16 +164,19 @@ def tile_list_measles_interchange_tracing_kernel(
             for piece in range(2):
                 src = w1_raw[2 * b + piece][:].rearrange("p j (m t) -> p m j t", t=4)
                 nc.scalar.copy(dealt[:, piece * QUART // 4 : (piece + 1) * QUART // 4], src)
-            deal(w_codes[1][:, cols], w2_raw[b][:])
-            nc.vector.quantize_mx(out=w_codes[0][:, cols].bitcast(FP8X4), scales=w_sc[0][:, cols], in_=w1_bf[:])
+            deal(w_codes[1, b][:], w2_raw[b][:])
+            nc.vector.quantize_mx(out=w_codes[0, b][:].bitcast(FP8X4), scales=w_sc[0][:, cols], in_=w1_bf[:])
 
-        prepare_weights(0)
-        gather(v_sc, table_sc, 0, 1, placed([P, HALF], U8, "sc1_0", W1_RAW_AT))
         deal(w_sc[1][:], w2_sc_raw[:])
-        gather(v_sc, table_sc, 1, 1, placed([P, HALF], U8, "sc1_1", W2_SC_AT))
-        gather(v_words, table, 0, 1, placed([P, HALF], U16, "words1_0", W2_SC_AT + HALF))
+        prepare_weights(0)
+        carry_scales(1, gather_scales(1, placed([P, 2, HALF], U8, "picked1", W1_BF_AT)))
+        load_given(0, 0, 2, NT)
+        load_given(1, 0, 0, NT)
+        for x in range(2):
+            load_given(x, 1, 0, NT)
         prepare_weights(1)
-        gather(v_words, table, 1, 1, placed([P, HALF], U16, "words1_1", W1_BF_AT + 8 * HALF))
+        for k in range(2):
+            gather(v_words, table, k, 1, placed([P, HALF], U16, "words1_%d" % k, W1_BF_AT + (8 + 2 * k) * HALF))
 
         def first_product(half, b, sig=None):
             if sig is None:
@@ -159,7 +186,7 @@ def tile_list_measles_interchange_tracing_kernel(
             def one_pass(t, k, first):
                 wc = slice(b * HALF + t * P, b * HALF + (t + 1) * P)
                 nc.tensor.matmul_mx(
-                    out=accs[t][:], lhsT=w_codes[k][:, wc].bitcast(FP8X4), lhsT_scale=w_sc[k][:, wc],
+                    out=accs[t][:], lhsT=w_codes[k, b][:, t * P : (t + 1) * P].bitcast(FP8X4), lhsT_scale=w_sc[k][:, wc],
                     rhs=v_words[k, half].bitcast(FP4X4), rhs_scale=v_sc[k, half], start=first, stop=not first)
 
             first_unit = half == 0 and b == 0
@@ -210,12 +237,12 @@ def tile_list_measles_interchange_tracing_kernel(
         def weigh(acc, half, rows, cols):
             prod = res.tile([P, HALF], F32, name="prod", bufs=NT + NT // 2)
             shaped = prod[:].rearrange("p (n j) -> p n j", n=rows.stop - rows.start)
-            nc.vector.tensor_tensor(shaped, given[0, half][:, rows, cols], acc, ALU.mult)
+            nc.vector.tensor_tensor(shaped, given_rows(0, half, rows, cols), acc, ALU.mult)
             return shaped, half, rows, cols
 
         def subtract(engine, prod, half, rows, cols):
             score = scores[half, cols.start][:, rows]
-            engine.tensor_tensor(score, given[1, half][:, rows, cols], prod, ALU.subtract)
+            engine.tensor_tensor(score, given_rows(1, half, rows, cols), prod, ALU.subtract)
             queue = nc.scalar if engine is nc.vector and half == 1 else nc.sync
             queue.dma_start(out_v[:, rows, half * HALF + cols.start : half * HALF + cols.stop], score)
 

@@ -18,14 +18,20 @@ ACT = mybir.ActivationFunctionType
 ALU = mybir.AluOpType
 
 P = 128
+KIB = 1024
 HALF = 512
 QUART = 256
 NT = N // P
 ROWS_AT = P - 16
-SCALAR_SHARE = 128
+VECTOR_SHARE = (128, 192)
+GPSIMD_SHARE = 256
+SIG_AT = 50 * KIB
+TABLE_AT = 58 * KIB
 W1_RAW_AT = 0
-W1_BF_AT = 4 * 16 * QUART
-LAST_BF_AT = W1_BF_AT + 16 * HALF
+W1_BF_AT = 16 * KIB
+H_BF_AT = 28 * KIB
+LAST_HOURS_AT = 38 * KIB
+PROD_AT = 46 * KIB
 
 
 def tile_list_measles_interchange_tracing_kernel(
@@ -36,9 +42,7 @@ def tile_list_measles_interchange_tracing_kernel(
     with ExitStack() as ctx:
         lists = ctx.enter_context(tc.tile_pool(name="lists", bufs=1))
         keep = ctx.enter_context(tc.tile_pool(name="keep", bufs=1))
-        ring = ctx.enter_context(tc.tile_pool(name="ring", bufs=4))
         shared = ctx.enter_context(tc.tile_pool(name="shared", bufs=1))
-        res = ctx.enter_context(tc.tile_pool(name="res", bufs=6))
         psum_consts = ctx.enter_context(tc.psum_pool(name="psum_consts", bufs=1))
         psum_four = ctx.enter_context(tc.psum_pool(name="psum_four", bufs=4))
         psum_three = ctx.enter_context(tc.psum_pool(name="psum_three", bufs=3))
@@ -63,7 +67,7 @@ def tile_list_measles_interchange_tracing_kernel(
             for r in range(4):
                 nc.sync.dma_start(plane[r:P:32].bitcast(I32), rows[r:16:4].bitcast(I32))
 
-        table = held([P, T], U16, "table")
+        table = placed([P, T], U16, "table", TABLE_AT)
         table_sc = held([P, T], U8, "table_sc")
         nc.sync.dma_start(table_sc[ROWS_AT:P].bitcast(I32), tab_scales[0].bitcast(I32))
         w2_sc_raw = held([P, H], U8, "w2_sc_raw")
@@ -72,9 +76,10 @@ def tile_list_measles_interchange_tracing_kernel(
         nc.gpsimd.memset(const_rows[:], 0.0)
         nc.gpsimd.memset(table_sc[0:96].bitcast(I32), 0)
         nc.vector.memset(table_sc[96:ROWS_AT].bitcast(I32), 0)
-        planes = [held([P, 2, HALF], U8, "plane%d" % half) for half in range(2)]
-        for plane in planes:
-            nc.vector.memset(plane[:].rearrange("p k c -> p (k c)").bitcast(I32), 0)
+        plane_early = held([P, 3 * HALF], U8, "plane_early")
+        plane_late = held([P, HALF], U8, "plane_late")
+        nc.vector.memset(plane_early[:].bitcast(I32), 0)
+        nc.vector.memset(plane_late[:].bitcast(I32), 0)
         nc.sync.dma_start(table[:].bitcast(I32), tab_words[0].bitcast(I32))
         nc.sync.dma_start(const_rows[0:2, :], gain.rearrange("(b c) -> b c", b=2))
         nc.sync.dma_start(const_rows[2:4, :], bias.rearrange("(b c) -> b c", b=2))
@@ -107,26 +112,23 @@ def tile_list_measles_interchange_tracing_kernel(
         consts = held([P, 4, 4], F32, "consts")
         nc.scalar.copy(consts[:], consts_ps[:, 0:4, :])
 
-        v_words, v_sc = {}, {}
+        v_words = {}
+        v_sc = {(0, 0): plane_early[:, 0:HALF], (0, 1): plane_early[:, HALF:S], (1, 0): plane_early[:, S : S + HALF],
+                (1, 1): plane_late[:]}
 
         def gather(store, window, k, half, dst):
             cols = slice(half * HALF // 16, (half + 1) * HALF // 16)
             store[k, half] = dst[:]
             nc.vector.tensor_copy(dst[:], window[:].indirect(both[k][:, cols]))
 
-        def gather_scales(half, picked):
-            cols = slice(half * HALF // 16, (half + 1) * HALF // 16)
-            for k in range(2):
-                nc.vector.tensor_copy(picked[:, k], table_sc[:].indirect(both[k][:, cols]))
-                v_sc[k, half] = planes[half][:, k]
-            return picked
-
-        def carry_scales(half, picked):
+        def carry(plane, picked):
             for r in range(4):
-                nc.sync.dma_start(planes[half][r:P:32].rearrange("p k c -> p (k c)").bitcast(I32),
-                                  picked[ROWS_AT + r : P : 4].rearrange("p k c -> p (k c)").bitcast(I32))
+                nc.sync.dma_start(plane[r:P:32].bitcast(I32), picked[ROWS_AT + r : P : 4].bitcast(I32))
 
-        carry_scales(0, gather_scales(0, held([P, 2, HALF], U8, "picked0")))
+        picked_early = held([P, 3 * HALF], U8, "picked_early")
+        nc.vector.tensor_copy(picked_early[:, 0:S], table_sc[:].indirect(list_a[:]))
+        nc.vector.tensor_copy(picked_early[:, S : S + HALF], table_sc[:].indirect(list_b[:, 0 : HALF // 16]))
+        carry(plane_early, picked_early)
         load_w1(2)
         load_w1(3)
         load_w2(1)
@@ -135,18 +137,18 @@ def tile_list_measles_interchange_tracing_kernel(
         nc.sync.dma_start(w3_codes[:].bitcast(I32), w3_words.rearrange("a p c -> p a c").bitcast(I32))
         given = {}
 
-        def load_given(x, half, n0, n1):
-            tile = held([P, n1 - n0, HALF], F32, "given%d%d%d" % (x, half, n0))
+        def load_given(x, n0, n1, tile=None):
+            if tile is None:
+                tile = held([P, n1 - n0, S], F32, "given%d%d" % (x, n0))
             rows = (hours, sus)[x].rearrange("(n p) j -> p n j", p=P)
-            nc.sync.dma_start(tile[:], rows[:, n0:n1, half * HALF : (half + 1) * HALF])
+            nc.sync.dma_start(tile[:], rows[:, n0:n1, :])
             for n in range(n0, n1):
-                given[x, half, n] = tile, n - n0
+                given[x, n] = tile[:, n - n0]
 
-        def given_rows(x, half, rows, cols):
-            tile, first = given[x, half, rows.start]
-            return tile[:, first : first + rows.stop - rows.start, cols]
+        def given_row(x, half, n):
+            return given[x, n][:, half * HALF : (half + 1) * HALF]
 
-        load_given(0, 0, 0, 2)
+        load_given(0, 0, 1)
         for k in range(2):
             gather(v_words, table, k, 0, held([P, HALF], U16, "words0_%d" % k))
 
@@ -163,143 +165,148 @@ def tile_list_measles_interchange_tracing_kernel(
             dealt = w1_bf[:].rearrange("p (t m j) -> p m j t", t=4, j=4)
             for piece in range(2):
                 src = w1_raw[2 * b + piece][:].rearrange("p j (m t) -> p m j t", t=4)
-                nc.scalar.copy(dealt[:, piece * QUART // 4 : (piece + 1) * QUART // 4], src)
+                copy = nc.vector.tensor_copy if 2 * b + piece == 3 else nc.scalar.copy
+                copy(dealt[:, piece * QUART // 4 : (piece + 1) * QUART // 4], src)
             deal(w_codes[1, b][:], w2_raw[b][:])
             nc.vector.quantize_mx(out=w_codes[0, b][:].bitcast(FP8X4), scales=w_sc[0][:, cols], in_=w1_bf[:])
 
         deal(w_sc[1][:], w2_sc_raw[:])
         prepare_weights(0)
-        carry_scales(1, gather_scales(1, placed([P, 2, HALF], U8, "picked1", W1_BF_AT)))
-        load_given(0, 0, 2, NT)
-        load_given(1, 0, 0, NT)
-        for x in range(2):
-            load_given(x, 1, 0, NT)
+        picked_late = placed([P, HALF], U8, "picked_late", W1_BF_AT)
+        nc.vector.tensor_copy(picked_late[:], table_sc[:].indirect(list_b[:, HALF // 16 : S // 16]))
+        carry(plane_late, picked_late)
+        load_given(0, 1, 2)
+        load_given(0, 2, 4)
+        load_given(1, 0, 2)
+        load_given(0, 4, 6, placed([P, 2, S], F32, "last_hours", LAST_HOURS_AT))
+        load_given(1, 2, 4)
+        load_given(1, 4, 6)
         prepare_weights(1)
         for k in range(2):
             gather(v_words, table, k, 1, placed([P, HALF], U16, "words1_%d" % k, W1_BF_AT + (8 + 2 * k) * HALF))
 
-        def first_product(half, b, sig=None):
-            if sig is None:
-                sig = ring.tile([P, 4, HALF], F32, name="sig")
+        def first_product(half, b, sig):
             accs = [psum_four.tile([P, HALF], F32, name="acc") for t in range(4)]
 
-            def one_pass(t, k, first):
+            def one_pass(t, k, start):
                 wc = slice(b * HALF + t * P, b * HALF + (t + 1) * P)
                 nc.tensor.matmul_mx(
                     out=accs[t][:], lhsT=w_codes[k, b][:, t * P : (t + 1) * P].bitcast(FP8X4), lhsT_scale=w_sc[k][:, wc],
-                    rhs=v_words[k, half].bitcast(FP4X4), rhs_scale=v_sc[k, half], start=first, stop=not first)
+                    rhs=v_words[k, half].bitcast(FP4X4), rhs_scale=v_sc[k, half], start=start, stop=not start)
 
-            first_unit = half == 0 and b == 0
-            if first_unit:
-                for t in range(4):
-                    one_pass(t, 0, True)
+            ahead = 2 if half == 0 and b == 0 else 0
+            for t in range(ahead):
+                one_pass(t, 1, True)
             for t in range(4):
-                if not first_unit:
-                    one_pass(t, 0, True)
-                one_pass(t, 1, False)
+                if t >= ahead:
+                    one_pass(t, 1, True)
+                one_pass(t, 0, False)
                 nc.scalar.activation(sig[:, t, :], accs[t][:], ACT.Sigmoid, bias=consts[:, 2 + b, t : t + 1])
             return sig
 
-        def gain_on_vector(dst, sig, b, c0, c1):
+        h_bf = {(0, 0): placed([P, 4 * HALF], BF16, "h_bf00", TABLE_AT), (0, 1): held([P, 4 * HALF], BF16, "h_bf01")}
+        for b in range(2):
+            h_bf[1, b] = placed([P, 4 * HALF], BF16, "h_bf1%d" % b, H_BF_AT + 5 * KIB * b)
+        units = [(half, b) for half in range(2) for b in range(2)]
+        h_codes = {(0, 1): held([P, HALF], U32, "h_codes01")}
+        h_sc = {u: held([P, HALF], U8, "h_sc%d%d" % u) for u in units}
+        sig = {}
+
+        def gain_on_vector(half, b, c0, c1):
             nc.vector.tensor_tensor(
-                dst.rearrange("p (c i t) -> p c t i", i=2, t=4),
-                sig[:, :, c0:c1].rearrange("p t (c i) -> p c t i", i=2),
+                h_bf[half, b][:, 4 * c0 : 4 * c1].rearrange("p (c i t) -> p c t i", i=2, t=4),
+                sig[half, b][:, :, c0:c1].rearrange("p t (c i) -> p c t i", i=2),
                 consts_ps[:, b, :].unsqueeze(1).unsqueeze(3).to_broadcast([P, (c1 - c0) // 2, 4, 2]), ALU.mult)
 
-        def interleave_on_scalar(dst, h_rows):
-            nc.scalar.copy(dst.rearrange("p (c i t) -> p c t i", i=4, t=4),
+        def gain_on_gpsimd(half, b, c0, c1):
+            nc.gpsimd.tensor_tensor(
+                h_bf[half, b][:, 4 * c0 : 4 * c1].rearrange("p (c t) -> p c t", t=4),
+                sig[half, b][:, :, c0:c1].rearrange("p t c -> p c t"),
+                consts[:, b, :].unsqueeze(1).to_broadcast([P, c1 - c0, 4]), ALU.mult)
+
+        def gain_on_scalar(half, b, c0, c1):
+            h_rows = held([P, 4, c1 - c0], BF16, "h_rows%d%d" % (half, b))
+            for t in range(4):
+                nc.scalar.activation(h_rows[:, t, :], sig[half, b][:, t, c0:c1], ACT.Copy, scale=consts[:, b, t : t + 1])
+            nc.scalar.copy(h_bf[half, b][:, 4 * c0 : 4 * c1].rearrange("p (c i t) -> p c t i", i=4, t=4),
                            h_rows[:].rearrange("p t (c i) -> p c t i", i=4))
 
-        def gain_on_scalar(dst, sig, b, c0, c1):
-            h_rows = ring.tile([P, 4, c1 - c0], BF16, name="h_rows")
-            for t in range(4):
-                nc.scalar.activation(h_rows[:, t, :], sig[:, t, c0:c1], ACT.Copy, scale=consts[:, b, t : t + 1])
-            interleave_on_scalar(dst, h_rows)
-
-        h_bf = [held([P, 4 * HALF], BF16, "h_bf%d" % i) for i in (0, 1, 3)]
-        h_bf.insert(2, placed([P, 4 * HALF], BF16, "h_bf2", LAST_BF_AT))
-        h_codes = [held([P, HALF], U32, "h_codes%d" % i) for i in range(4)]
-        h_sc = [held([P, HALF], U8, "h_sc%d" % i) for i in range(4)]
-
-        def quantise(i):
-            nc.vector.quantize_mx(out=h_codes[i][:].bitcast(FP8X4), scales=h_sc[i][:], in_=h_bf[i][:])
+        def quantise(half, b):
+            if half == 1:
+                h_codes[1, b] = placed([P, HALF], U32, "h_codes1%d" % b, PROD_AT + 2 * KIB * b)
+            nc.vector.quantize_mx(out=h_codes[half, b][:].bitcast(FP8X4), scales=h_sc[half, b][:], in_=h_bf[half, b][:])
 
         out_v = out.rearrange("(n p) j -> p n j", p=P)
-        scores = {(0, 0): held([P, NT, QUART], F32, "scores_first"), (1, 0): held([P, NT, HALF], F32, "scores_last")}
+        accs, prods = {}, {}
 
-        def one_pass(acc, n, b, i, c0, width, start, stop):
+        def second_pass(half, n, b, start):
             nc.tensor.matmul_mx(
-                out=acc, lhsT=w3_codes[:, b, 2 * P * n : 2 * P * (n + 1)].bitcast(FP4X4),
+                out=accs[half, n][:], lhsT=w3_codes[:, b, 2 * P * n : 2 * P * (n + 1)].bitcast(FP4X4),
                 lhsT_scale=w3_sc[:, b, P * n : P * (n + 1)],
-                rhs=h_codes[i][:, c0 : c0 + width].bitcast(FP8X4), rhs_scale=h_sc[i][:, c0 : c0 + width],
-                start=start, stop=stop)
+                rhs=h_codes[half, b][:].bitcast(FP8X4), rhs_scale=h_sc[half, b][:], start=start, stop=not start)
 
-        def weigh(acc, half, rows, cols):
-            prod = res.tile([P, HALF], F32, name="prod", bufs=NT + NT // 2)
-            shaped = prod[:].rearrange("p (n j) -> p n j", n=rows.stop - rows.start)
-            nc.vector.tensor_tensor(shaped, given_rows(0, half, rows, cols), acc, ALU.mult)
-            return shaped, half, rows, cols
+        def open_bank(half, n, pool):
+            accs[half, n] = pool.tile([P, HALF], F32, name="acc")
+            second_pass(half, n, 0, True)
 
-        def subtract(engine, prod, half, rows, cols):
-            score = scores[half, cols.start][:, rows]
-            engine.tensor_tensor(score, given_rows(1, half, rows, cols), prod, ALU.subtract)
-            queue = nc.scalar if engine is nc.vector and half == 1 else nc.sync
-            queue.dma_start(out_v[:, rows, half * HALF + cols.start : half * HALF + cols.stop], score)
-
-        def second_product_quarter(c, on_gpsimd):
-            left = []
-            for g in range(NT // 2):
-                acc = psum_three.tile([P, 2, QUART], F32, name="acc")
-                spots = [(b, u, m0) for b in range(2) for u in range(2) for m0 in range(0, QUART, P)]
-                for i, (b, u, m0) in enumerate(spots):
-                    one_pass(acc[:, u, m0 : m0 + P], 2 * g + u, b, c, b * QUART + m0, P, i == 0, i == len(spots) - 1)
-                weighed = weigh(acc[:], 0, slice(2 * g, 2 * g + 2), slice(c * QUART, (c + 1) * QUART))
-                if g < on_gpsimd:
-                    subtract(nc.gpsimd, *weighed)
+        def weigh(half, n):
+            second_pass(half, n, 1, False)
+            for c0, c1 in parts(half, n):
+                name = "prod%d%d_%d" % (half, n, c0)
+                if half == 0 and n in (2, 4) and c0 == 0:
+                    prods[half, n, c0] = placed([P, c1 - c0], F32, name, PROD_AT + KIB * (n - 2))
                 else:
-                    left.append(weighed)
-            return left
+                    prods[half, n, c0] = held([P, c1 - c0], F32, name)
+                nc.vector.tensor_tensor(prods[half, n, c0][:], given_row(0, half, n)[:, c0:c1], accs[half, n][:, c0:c1],
+                                        ALU.mult)
 
-        def second_product_half(ahead, on_gpsimd):
-            accs = [(psum_four if n < 4 else psum_three).tile([P, 1, HALF], F32, name="acc") for n in range(NT)]
-            for n in range(ahead):
-                one_pass(accs[n][:, 0], n, 1, 3, 0, HALF, True, False)
-            left = []
-            for n in range(NT):
-                if n >= ahead:
-                    one_pass(accs[n][:, 0], n, 1, 3, 0, HALF, True, False)
-                one_pass(accs[n][:, 0], n, 0, 2, 0, HALF, False, True)
-                weighed = weigh(accs[n][:], 1, slice(n, n + 1), slice(0, HALF))
-                if n < on_gpsimd:
-                    subtract(nc.gpsimd, *weighed)
-                else:
-                    left.append(weighed)
-            return left
+        def parts(half, n):
+            return ((0, QUART), (QUART, HALF)) if (half, n) == (0, 2) else ((0, HALF),)
 
-        def first_half_gain(c, b, sig):
-            gain_on_vector(h_bf[c][:, 4 * QUART * b : 4 * QUART * (b + 1)], sig, b, c * QUART, (c + 1) * QUART)
+        def subtract(engine, half, n, score, part=0):
+            c0, c1 = parts(half, n)[part]
+            engine.tensor_tensor(score, given_row(1, half, n)[:, c0:c1], prods[half, n, c0][:], ALU.subtract)
+            nc.sync.dma_start(out_v[:, n, half * HALF + c0 : half * HALF + c1], score)
 
-        sig00 = first_product(0, 0, placed([P, 4, HALF], F32, "sig00", W1_RAW_AT + 32 * QUART))
-        sig01 = first_product(0, 1)
-        first_half_gain(0, 0, sig00)
-        first_half_gain(1, 0, sig00)
-        sig10 = first_product(1, 0)
-        first_half_gain(0, 1, sig01)
-        quantise(0)
-        first_half_gain(1, 1, sig01)
-        quantise(1)
-        sig11 = first_product(1, 1)
-        left = second_product_quarter(0, 2)
-        gain_on_scalar(h_bf[3][:, 0 : 4 * SCALAR_SHARE], sig11, 1, 0, SCALAR_SHARE)
-        gain_on_scalar(h_bf[2][:], sig10, 0, 0, HALF)
-        gain_on_vector(h_bf[3][:, 4 * SCALAR_SHARE : 4 * HALF], sig11, 1, SCALAR_SHARE, HALF)
-        for weighed in left:
-            subtract(nc.vector, *weighed)
-        quantise(3)
-        left = second_product_quarter(1, 0)
-        quantise(2)
-        scores[0, QUART] = placed([P, NT, QUART], F32, "scores_second", LAST_BF_AT)
-        for weighed in left:
-            subtract(nc.gpsimd, *weighed)
-        for weighed in second_product_half(4, 0):
-            subtract(nc.vector, *weighed)
+        def own_score(half, n):
+            return held([P, parts(half, n)[0][1]], F32, "score%d%d" % (half, n))[:]
+
+        sig[0, 0] = first_product(0, 0, placed([P, 4, HALF], F32, "sig00", W1_RAW_AT + 4 * KIB))
+        sig[0, 1] = first_product(0, 1, placed([P, 4, HALF], F32, "sig01", SIG_AT))
+        gain_on_vector(0, 0, 0, HALF - GPSIMD_SHARE)
+        gain_on_gpsimd(0, 0, HALF - GPSIMD_SHARE, HALF)
+        sig[1, 0] = first_product(1, 0, held([P, 4, HALF], F32, "sig10"))
+        gain_on_vector(0, 1, 0, HALF)
+        h_codes[0, 0] = placed([P, HALF], U32, "h_codes00", SIG_AT)
+        quantise(0, 0)
+        quantise(0, 1)
+        sig[1, 1] = first_product(1, 1, held([P, 4, HALF], F32, "sig11"))
+        gain_on_vector(1, 0, 0, VECTOR_SHARE[0])
+        for n in range(2):
+            open_bank(0, n, psum_four)
+        for n in range(NT):
+            if n >= 2:
+                open_bank(0, n, psum_four)
+            weigh(0, n)
+            if n < 3:
+                subtract(nc.gpsimd, 0, n, own_score(0, n))
+        gain_on_vector(1, 1, 0, VECTOR_SHARE[1])
+        gain_on_scalar(1, 0, VECTOR_SHARE[0], HALF)
+        gain_on_scalar(1, 1, VECTOR_SHARE[1], HALF)
+        quantise(1, 0)
+        for n in range(3):
+            open_bank(1, n, psum_three)
+        subtract(nc.vector, 0, 2, placed([P, QUART], F32, "score02b", H_BF_AT - KIB + 32 * 2)[:], 1)
+        for n in (3, 4):
+            subtract(nc.vector, 0, n, placed([P, HALF], F32, "score0%d" % n, H_BF_AT + 64 + 2 * KIB * (n - 3))[:])
+        quantise(1, 1)
+        subtract(nc.vector, 0, 5, placed([P, HALF], F32, "score05", H_BF_AT + 5 * KIB)[:])
+        for n in range(NT):
+            if n >= 3:
+                open_bank(1, n, psum_three)
+            weigh(1, n)
+            if n < 2:
+                subtract(nc.gpsimd, 1, n, own_score(1, n))
+        last_scores = placed([P, NT - 2, HALF], F32, "last_scores", LAST_HOURS_AT)
+        for n in range(2, NT):
+            subtract(nc.vector, 1, n, last_scores[:, n - 2])

@@ -137,18 +137,19 @@ def tile_list_measles_interchange_tracing_kernel(
         nc.sync.dma_start(w3_codes[:].bitcast(I32), w3_words.rearrange("a p c -> p a c").bitcast(I32))
         given = {}
 
-        def load_given(x, n0, n1, tile=None):
+        def load_given(x, n0, n1, halves, tile=None):
             if tile is None:
-                tile = held([P, n1 - n0, S], F32, "given%d%d" % (x, n0))
+                tile = held([P, n1 - n0, len(halves) * HALF], F32, "given%d%d%d" % (x, n0, halves[0]))
             rows = (hours, sus)[x].rearrange("(n p) j -> p n j", p=P)
-            nc.sync.dma_start(tile[:], rows[:, n0:n1, :])
+            nc.sync.dma_start(tile[:], rows[:, n0:n1, halves[0] * HALF : (halves[-1] + 1) * HALF])
             for n in range(n0, n1):
-                given[x, n] = tile[:, n - n0]
+                for i, half in enumerate(halves):
+                    given[x, half, n] = tile[:, n - n0, i * HALF : (i + 1) * HALF]
 
         def given_row(x, half, n):
-            return given[x, n][:, half * HALF : (half + 1) * HALF]
+            return given[x, half, n]
 
-        load_given(0, 0, 1)
+        load_given(0, 0, 1, (0, 1))
         for k in range(2):
             gather(v_words, table, k, 0, held([P, HALF], U16, "words0_%d" % k))
 
@@ -175,12 +176,14 @@ def tile_list_measles_interchange_tracing_kernel(
         picked_late = placed([P, HALF], U8, "picked_late", W1_BF_AT)
         nc.vector.tensor_copy(picked_late[:], table_sc[:].indirect(list_b[:, HALF // 16 : S // 16]))
         carry(plane_late, picked_late)
-        load_given(0, 1, 2)
-        load_given(0, 2, 4)
-        load_given(1, 0, 2)
-        load_given(0, 4, 6, placed([P, 2, S], F32, "last_hours", LAST_HOURS_AT))
-        load_given(1, 2, 4)
-        load_given(1, 4, 6)
+        load_given(0, 1, 2, (0, 1))
+        load_given(0, 2, 4, (0, 1))
+        load_given(1, 0, 2, (0,))
+        load_given(0, 4, 6, (0, 1), placed([P, 2, S], F32, "last_hours", LAST_HOURS_AT))
+        load_given(1, 2, 4, (0,))
+        load_given(1, 4, 6, (0,))
+        load_given(1, 0, 2, (1,))
+        load_given(1, 2, 6, (1,))
         prepare_weights(1)
         for k in range(2):
             gather(v_words, table, k, 1, placed([P, HALF], U16, "words1_%d" % k, W1_BF_AT + (8 + 2 * k) * HALF))

@@ -23,8 +23,9 @@ HALF = 512
 QUART = 256
 NT = N // P
 ROWS_AT = P - 16
-VECTOR_SHARE = (128, 192)
+VECTOR_SHARE = (128, 208)
 GPSIMD_SHARE = 256
+TURNED = ((0, 3), (1, 2))
 SIG_AT = 50 * KIB
 TABLE_AT = 58 * KIB
 W1_RAW_AT = 0
@@ -59,6 +60,8 @@ def tile_list_measles_interchange_tracing_kernel(
 
         list_a = lists.tile([P, S // 16], U16, name="list_a")
         list_b = lists.tile([P, S // 16], U16, name="list_b")
+        table_sc = held([P, T], U8, "table_sc")
+        nc.sync.dma_start(table_sc[ROWS_AT:P].bitcast(I32), tab_scales[0].bitcast(I32))
         nc.sync.dma_start(list_a[:], offs)
         nc.sync.dma_start(list_b[:], offs2)
         both = (list_a, list_b)
@@ -68,14 +71,11 @@ def tile_list_measles_interchange_tracing_kernel(
                 nc.sync.dma_start(plane[r:P:32].bitcast(I32), rows[r:16:4].bitcast(I32))
 
         table = placed([P, T], U16, "table", TABLE_AT)
-        table_sc = held([P, T], U8, "table_sc")
-        nc.sync.dma_start(table_sc[ROWS_AT:P].bitcast(I32), tab_scales[0].bitcast(I32))
         w2_sc_raw = held([P, H], U8, "w2_sc_raw")
         nc.vector.memset(w2_sc_raw[:].bitcast(I32), 0)
         const_rows = held([P, HALF], F32, "const_rows")
         nc.gpsimd.memset(const_rows[:], 0.0)
-        nc.gpsimd.memset(table_sc[0:96].bitcast(I32), 0)
-        nc.vector.memset(table_sc[96:ROWS_AT].bitcast(I32), 0)
+        nc.gpsimd.memset(table_sc[0:ROWS_AT].bitcast(I32), 0)
         plane_early = held([P, 3 * HALF], U8, "plane_early")
         plane_late = held([P, HALF], U8, "plane_late")
         nc.vector.memset(plane_early[:].bitcast(I32), 0)
@@ -248,12 +248,34 @@ def tile_list_measles_interchange_tracing_kernel(
                 lhsT_scale=w3_sc[:, b, P * n : P * (n + 1)],
                 rhs=h_codes[half, b][:].bitcast(FP8X4), rhs_scale=h_sc[half, b][:], start=start, stop=not start)
 
-        def open_bank(half, n, pool):
+        def open_bank(half, n, pool, b=0):
             accs[half, n] = pool.tile([P, HALF], F32, name="acc")
-            second_pass(half, n, 0, True)
+            second_pass(half, n, b, True)
 
-        def weigh(half, n):
-            second_pass(half, n, 1, False)
+        def turn_and_add(half, n, bank):
+            for i, rows in enumerate((given_row(1, half, n), prods[half, n, 0])):
+                for c in range(0, HALF, P):
+                    nc.tensor.matmul(bank[:, c : c + P], rows[:, c : c + P], identity[:], is_transpose=True,
+                                     start=i == 0 and c == 0, stop=i == 1 and c == HALF - P)
+            turned = held([P, HALF], F32, "turned%d" % half)
+            nc.scalar.copy(turned[:], bank[:])
+            return turned
+
+        def turn_back_and_store(half, n, turned):
+            bank = psum_consts.tile([P, HALF], F32, name="consts_ps")
+            for c in range(0, HALF, P):
+                nc.tensor.transpose(bank[:, c : c + P], turned[:, c : c + P], identity[:])
+            score = own_score(half, n)
+            nc.scalar.copy(score, bank[:])
+            nc.sync.dma_start(out_v[:, n, half * HALF : (half + 1) * HALF], score)
+
+        def weigh(half, n, b=1):
+            second_pass(half, n, b, False)
+            if (half, n) in TURNED:
+                prods[half, n, 0] = held([P, HALF], F32, "prod%d%d" % (half, n))
+                nc.vector.scalar_tensor_tensor(prods[half, n, 0][:], accs[half, n][:], -1.0, given_row(0, half, n),
+                                               ALU.mult, ALU.mult)
+                return
             for c0, c1 in parts(half, n):
                 name = "prod%d%d_%d" % (half, n, c0)
                 if half == 0 and n in (2, 4) and c0 == 0:
@@ -296,20 +318,23 @@ def tile_list_measles_interchange_tracing_kernel(
         gain_on_vector(1, 1, 0, VECTOR_SHARE[1])
         gain_on_scalar(1, 0, VECTOR_SHARE[0], HALF)
         gain_on_scalar(1, 1, VECTOR_SHARE[1], HALF)
+        turned = turn_and_add(0, 3, psum_four.tile([P, HALF], F32, name="acc"))
         quantise(1, 0)
         for n in range(3):
             open_bank(1, n, psum_three)
         subtract(nc.vector, 0, 2, placed([P, QUART], F32, "score02b", H_BF_AT - KIB + 32 * 2)[:], 1)
-        for n in (3, 4):
-            subtract(nc.vector, 0, n, placed([P, HALF], F32, "score0%d" % n, H_BF_AT + 64 + 2 * KIB * (n - 3))[:])
+        subtract(nc.vector, 0, 4, placed([P, HALF], F32, "score04", H_BF_AT + 64)[:])
         quantise(1, 1)
         subtract(nc.vector, 0, 5, placed([P, HALF], F32, "score05", H_BF_AT + 5 * KIB)[:])
         for n in range(NT):
+            if n == 3:
+                turn_back_and_store(0, 3, turned)
             if n >= 3:
-                open_bank(1, n, psum_three)
-            weigh(1, n)
+                open_bank(1, n, psum_four, 1)
+            weigh(1, n, 1 if n < 3 else 0)
             if n < 2:
                 subtract(nc.gpsimd, 1, n, own_score(1, n))
-        last_scores = placed([P, NT - 2, HALF], F32, "last_scores", LAST_HOURS_AT)
-        for n in range(2, NT):
-            subtract(nc.vector, 1, n, last_scores[:, n - 2])
+        turn_back_and_store(1, 2, turn_and_add(1, 2, psum_four.tile([P, HALF], F32, name="acc")))
+        last_scores = placed([P, NT - 3, HALF], F32, "last_scores", LAST_HOURS_AT)
+        for n in range(3, NT):
+            subtract(nc.vector, 1, n, last_scores[:, n - 3])

@@ -23,16 +23,18 @@ HALF = 512
 QUART = 256
 NT = N // P
 ROWS_AT = P - 16
-VECTOR_SHARE = (128, 208)
+SCALAR_SHARE = 160
 GPSIMD_SHARE = 256
-TURNED = ((0, 3), (1, 2))
+TURNED = ((0, 3), (1, 2), (1, 3))
+FILL_AT = 24 * KIB
 SIG_AT = 50 * KIB
 TABLE_AT = 58 * KIB
+ROWS_BF_AT = 66 * KIB
 W1_RAW_AT = 0
 W1_BF_AT = 16 * KIB
 H_BF_AT = 28 * KIB
 LAST_HOURS_AT = 38 * KIB
-PROD_AT = 46 * KIB
+PROD_AT = 76 * KIB
 
 
 def tile_list_measles_interchange_tracing_kernel(
@@ -44,9 +46,10 @@ def tile_list_measles_interchange_tracing_kernel(
         lists = ctx.enter_context(tc.tile_pool(name="lists", bufs=1))
         keep = ctx.enter_context(tc.tile_pool(name="keep", bufs=1))
         shared = ctx.enter_context(tc.tile_pool(name="shared", bufs=1))
-        psum_consts = ctx.enter_context(tc.psum_pool(name="psum_consts", bufs=1))
-        psum_four = ctx.enter_context(tc.psum_pool(name="psum_four", bufs=4))
-        psum_three = ctx.enter_context(tc.psum_pool(name="psum_three", bufs=3))
+        psum = ctx.enter_context(tc.psum_pool(name="psum", bufs=1))
+
+        def bank(i, shape=(P, HALF)):
+            return psum.tile(list(shape), F32, name="bank%d" % i, tag="bank%d" % i)
 
         def held(shape, dtype, name, tag=None):
             return keep.tile(shape, dtype, name=name, tag=tag or name, align_bytes=64)
@@ -106,7 +109,7 @@ def tile_list_measles_interchange_tracing_kernel(
         load_w1(1)
         load_w2(0)
 
-        consts_ps = psum_consts.tile([P, P, 4], F32, name="consts_ps")
+        consts_ps = bank(7, (P, P, 4))
         for t in range(4):
             nc.tensor.transpose(consts_ps[:, :, t], const_rows[:, t:HALF:4], identity[:])
         consts = held([P, 4, 4], F32, "consts")
@@ -189,7 +192,7 @@ def tile_list_measles_interchange_tracing_kernel(
             gather(v_words, table, k, 1, placed([P, HALF], U16, "words1_%d" % k, W1_BF_AT + (8 + 2 * k) * HALF))
 
         def first_product(half, b, sig):
-            accs = [psum_four.tile([P, HALF], F32, name="acc") for t in range(4)]
+            accs = [bank((4 * (2 * half + b) + t) % 7) for t in range(4)]
 
             def one_pass(t, k, start):
                 wc = slice(b * HALF + t * P, b * HALF + (t + 1) * P)
@@ -211,7 +214,7 @@ def tile_list_measles_interchange_tracing_kernel(
         for b in range(2):
             h_bf[1, b] = placed([P, 4 * HALF], BF16, "h_bf1%d" % b, H_BF_AT + 5 * KIB * b)
         units = [(half, b) for half in range(2) for b in range(2)]
-        h_codes = {(0, 1): held([P, HALF], U32, "h_codes01")}
+        h_codes = {}
         h_sc = {u: held([P, HALF], U8, "h_sc%d%d" % u) for u in units}
         sig = {}
 
@@ -228,19 +231,18 @@ def tile_list_measles_interchange_tracing_kernel(
                 consts[:, b, :].unsqueeze(1).to_broadcast([P, c1 - c0, 4]), ALU.mult)
 
         def gain_on_scalar(half, b, c0, c1):
-            h_rows = held([P, 4, c1 - c0], BF16, "h_rows%d%d" % (half, b))
+            h_rows = placed([P, 4, c1 - c0], BF16, "h_rows%d" % b, ROWS_BF_AT + 4 * KIB * b)
             for t in range(4):
                 nc.scalar.activation(h_rows[:, t, :], sig[half, b][:, t, c0:c1], ACT.Copy, scale=consts[:, b, t : t + 1])
             nc.scalar.copy(h_bf[half, b][:, 4 * c0 : 4 * c1].rearrange("p (c i t) -> p c t i", i=4, t=4),
                            h_rows[:].rearrange("p t (c i) -> p c t i", i=4))
 
-        def quantise(half, b):
-            if half == 1:
-                h_codes[1, b] = placed([P, HALF], U32, "h_codes1%d" % b, PROD_AT + 2 * KIB * b)
-            nc.vector.quantize_mx(out=h_codes[half, b][:].bitcast(FP8X4), scales=h_sc[half, b][:], in_=h_bf[half, b][:])
+        def quantise(half, b, codes):
+            h_codes[half, b] = codes
+            nc.vector.quantize_mx(out=codes[:].bitcast(FP8X4), scales=h_sc[half, b][:], in_=h_bf[half, b][:])
 
         out_v = out.rearrange("(n p) j -> p n j", p=P)
-        accs, prods = {}, {}
+        accs, prods, turned = {}, {}, {}
 
         def second_pass(half, n, b, start):
             nc.tensor.matmul_mx(
@@ -248,53 +250,46 @@ def tile_list_measles_interchange_tracing_kernel(
                 lhsT_scale=w3_sc[:, b, P * n : P * (n + 1)],
                 rhs=h_codes[half, b][:].bitcast(FP8X4), rhs_scale=h_sc[half, b][:], start=start, stop=not start)
 
-        def open_bank(half, n, pool, b=0):
-            accs[half, n] = pool.tile([P, HALF], F32, name="acc")
+        def open_bank(half, n, i, b=0):
+            accs[half, n] = bank(i)
             second_pass(half, n, b, True)
 
-        def turn_and_add(half, n, bank):
-            for i, rows in enumerate((given_row(1, half, n), prods[half, n, 0])):
-                for c in range(0, HALF, P):
-                    nc.tensor.matmul(bank[:, c : c + P], rows[:, c : c + P], identity[:], is_transpose=True,
-                                     start=i == 0 and c == 0, stop=i == 1 and c == HALF - P)
-            turned = held([P, HALF], F32, "turned%d" % half)
-            nc.scalar.copy(turned[:], bank[:])
-            return turned
-
-        def turn_back_and_store(half, n, turned):
-            bank = psum_consts.tile([P, HALF], F32, name="consts_ps")
-            for c in range(0, HALF, P):
-                nc.tensor.transpose(bank[:, c : c + P], turned[:, c : c + P], identity[:])
-            score = own_score(half, n)
-            nc.scalar.copy(score, bank[:])
-            nc.sync.dma_start(out_v[:, n, half * HALF : (half + 1) * HALF], score)
-
-        def weigh(half, n, b=1):
+        def weigh(half, n, at=None, b=1):
             second_pass(half, n, b, False)
+            name = "prod%d%d" % (half, n)
+            prods[half, n] = held([P, HALF], F32, name) if at is None else placed([P, HALF], F32, name, at)
             if (half, n) in TURNED:
-                prods[half, n, 0] = held([P, HALF], F32, "prod%d%d" % (half, n))
-                nc.vector.scalar_tensor_tensor(prods[half, n, 0][:], accs[half, n][:], -1.0, given_row(0, half, n),
+                nc.vector.scalar_tensor_tensor(prods[half, n][:], accs[half, n][:], -1.0, given_row(0, half, n),
                                                ALU.mult, ALU.mult)
-                return
-            for c0, c1 in parts(half, n):
-                name = "prod%d%d_%d" % (half, n, c0)
-                if half == 0 and n in (2, 4) and c0 == 0:
-                    prods[half, n, c0] = placed([P, c1 - c0], F32, name, PROD_AT + KIB * (n - 2))
-                else:
-                    prods[half, n, c0] = held([P, c1 - c0], F32, name)
-                nc.vector.tensor_tensor(prods[half, n, c0][:], given_row(0, half, n)[:, c0:c1], accs[half, n][:, c0:c1],
-                                        ALU.mult)
+            else:
+                nc.vector.tensor_tensor(prods[half, n][:], given_row(0, half, n), accs[half, n][:], ALU.mult)
 
-        def parts(half, n):
-            return ((0, QUART), (QUART, HALF)) if (half, n) == (0, 2) else ((0, HALF),)
+        def store(half, n, score):
+            nc.sync.dma_start(out_v[:, n, half * HALF : (half + 1) * HALF], score[:])
 
-        def subtract(engine, half, n, score, part=0):
-            c0, c1 = parts(half, n)[part]
-            engine.tensor_tensor(score, given_row(1, half, n)[:, c0:c1], prods[half, n, c0][:], ALU.subtract)
-            nc.sync.dma_start(out_v[:, n, half * HALF + c0 : half * HALF + c1], score)
+        def subtract(engine, half, n, at=None, c0=0, c1=HALF):
+            name = "score%d%d_%d" % (half, n, c0)
+            score = held([P, c1 - c0], F32, name) if at is None else placed([P, c1 - c0], F32, name, at)
+            engine.tensor_tensor(score[:], given_row(1, half, n)[:, c0:c1], prods[half, n][:, c0:c1], ALU.subtract)
+            nc.sync.dma_start(out_v[:, n, half * HALF + c0 : half * HALF + c1], score[:])
 
-        def own_score(half, n):
-            return held([P, parts(half, n)[0][1]], F32, "score%d%d" % (half, n))[:]
+        def turn_and_add(half, n, i):
+            total = bank(i)
+            for x, rows in enumerate((given_row(1, half, n), prods[half, n])):
+                for c in range(0, HALF, P):
+                    nc.tensor.matmul(total[:, c : c + P], rows[:, c : c + P], identity[:], is_transpose=True,
+                                     start=x == 0 and c == 0, stop=x == 1 and c == HALF - P)
+            name = "turned%d%d" % (half, n)
+            turned[half, n] = held([P, HALF], F32, name) if half else placed([P, HALF], F32, name, ROWS_BF_AT + 4 * KIB)
+            nc.scalar.copy(turned[half, n][:], total[:])
+
+        def turn_back(half, n, i):
+            total = bank(i)
+            for c in range(0, HALF, P):
+                nc.tensor.transpose(total[:, c : c + P], turned[half, n][:, c : c + P], identity[:])
+            score = held([P, HALF], F32, "score%d%d" % (half, n))
+            nc.scalar.copy(score[:], total[:])
+            store(half, n, score)
 
         sig[0, 0] = first_product(0, 0, placed([P, 4, HALF], F32, "sig00", W1_RAW_AT + 4 * KIB))
         sig[0, 1] = first_product(0, 1, placed([P, 4, HALF], F32, "sig01", SIG_AT))
@@ -302,39 +297,40 @@ def tile_list_measles_interchange_tracing_kernel(
         gain_on_gpsimd(0, 0, HALF - GPSIMD_SHARE, HALF)
         sig[1, 0] = first_product(1, 0, held([P, 4, HALF], F32, "sig10"))
         gain_on_vector(0, 1, 0, HALF)
-        h_codes[0, 0] = placed([P, HALF], U32, "h_codes00", SIG_AT)
-        quantise(0, 0)
-        quantise(0, 1)
+        quantise(0, 0, placed([P, HALF], U32, "h_codes00", SIG_AT))
+        quantise(0, 1, held([P, HALF], U32, "h_codes01"))
+        gain_on_vector(1, 0, 0, HALF - SCALAR_SHARE)
+        gain_on_scalar(1, 0, HALF - SCALAR_SHARE, HALF)
         sig[1, 1] = first_product(1, 1, held([P, 4, HALF], F32, "sig11"))
-        gain_on_vector(1, 0, 0, VECTOR_SHARE[0])
-        for n in range(2):
-            open_bank(0, n, psum_four)
+        gain_on_scalar(1, 1, 0, HALF)
+        open_bank(0, 0, 2)
+        open_bank(0, 1, 3)
+        weigh(0, 0)
+        quantise(1, 0, held([P, HALF], U32, "h_codes10"))
+        subtract(nc.gpsimd, 0, 0, H_BF_AT)
+        weigh(0, 1, PROD_AT)
+        subtract(nc.gpsimd, 0, 1)
+        for n in range(2, NT):
+            open_bank(0, n, (n + 2) % 7)
+            weigh(0, n, FILL_AT if n == 4 else None)
+        for n, i in enumerate((1, 2, 3, 4)):
+            open_bank(1, n, i)
+        turn_and_add(0, 3, 7)
+        open_bank(1, 4, 6)
+        open_bank(1, 5, 0)
+        subtract(nc.vector, 0, 2, PROD_AT - 2 * KIB + 64)
+        subtract(nc.vector, 0, 4, PROD_AT + 64)
+        quantise(1, 1, placed([P, HALF], U32, "h_codes11", FILL_AT))
+        subtract(nc.vector, 0, 5, H_BF_AT + 5 * KIB)
         for n in range(NT):
-            if n >= 2:
-                open_bank(0, n, psum_four)
-            weigh(0, n)
-            if n < 3:
-                subtract(nc.gpsimd, 0, n, own_score(0, n))
-        gain_on_vector(1, 1, 0, VECTOR_SHARE[1])
-        gain_on_scalar(1, 0, VECTOR_SHARE[0], HALF)
-        gain_on_scalar(1, 1, VECTOR_SHARE[1], HALF)
-        turned = turn_and_add(0, 3, psum_four.tile([P, HALF], F32, name="acc"))
-        quantise(1, 0)
-        for n in range(3):
-            open_bank(1, n, psum_three)
-        subtract(nc.vector, 0, 2, placed([P, QUART], F32, "score02b", H_BF_AT - KIB + 32 * 2)[:], 1)
-        subtract(nc.vector, 0, 4, placed([P, HALF], F32, "score04", H_BF_AT + 64)[:])
-        quantise(1, 1)
-        subtract(nc.vector, 0, 5, placed([P, HALF], F32, "score05", H_BF_AT + 5 * KIB)[:])
-        for n in range(NT):
-            if n == 3:
-                turn_back_and_store(0, 3, turned)
-            if n >= 3:
-                open_bank(1, n, psum_four, 1)
-            weigh(1, n, 1 if n < 3 else 0)
+            weigh(1, n)
             if n < 2:
-                subtract(nc.gpsimd, 1, n, own_score(1, n))
-        turn_back_and_store(1, 2, turn_and_add(1, 2, psum_four.tile([P, HALF], F32, name="acc")))
-        last_scores = placed([P, NT - 3, HALF], F32, "last_scores", LAST_HOURS_AT)
-        for n in range(3, NT):
-            subtract(nc.vector, 1, n, last_scores[:, n - 3])
+                subtract(nc.gpsimd, 1, n)
+            if n == 2:
+                turn_back(0, 3, 5)
+        turn_and_add(1, 2, 1)
+        turn_and_add(1, 3, 2)
+        turn_back(1, 2, 7)
+        turn_back(1, 3, 5)
+        for n in (4, 5):
+            subtract(nc.vector, 1, n, LAST_HOURS_AT + 2 * KIB * (n - 4))

@@ -57,9 +57,10 @@ def tile_list_measles_interchange_tracing_kernel(
         def placed(shape, dtype, name, offset):
             return shared.tile(shape, dtype, name=name, offset=offset, align_bytes=64)
 
-        warm = held([P, 16], F32, "warm")
-        nc.gpsimd.memset(warm[:, 0:1], 0.0)
-        nc.scalar.activation(warm[:, 8:9], warm[:, 0:1], ACT.Sigmoid)
+        identity = held([P, P], F32, "identity")
+        make_identity(nc, identity[:])
+        warm = held([P, 8], F32, "warm")
+        nc.scalar.activation(warm[:, 0:1], identity[:, 0:1], ACT.Sigmoid)
 
         list_a = lists.tile([P, S // 16], U16, name="list_a")
         list_b = lists.tile([P, S // 16], U16, name="list_b")
@@ -77,8 +78,8 @@ def tile_list_measles_interchange_tracing_kernel(
         w2_sc_raw = held([P, H], U8, "w2_sc_raw")
         nc.vector.memset(w2_sc_raw[:].bitcast(I32), 0)
         const_rows = held([P, HALF], F32, "const_rows")
-        nc.gpsimd.memset(const_rows[:], 0.0)
-        nc.gpsimd.memset(table_sc[0:ROWS_AT].bitcast(I32), 0)
+        nc.vector.memset(const_rows[:], 0.0)
+        nc.vector.memset(table_sc[0:ROWS_AT].bitcast(I32), 0)
         plane_early = held([P, 3 * HALF], U8, "plane_early")
         plane_late = held([P, HALF], U8, "plane_late")
         nc.vector.memset(plane_early[:].bitcast(I32), 0)
@@ -90,8 +91,6 @@ def tile_list_measles_interchange_tracing_kernel(
 
         w3_sc = held([P, 2, N], U8, "w3_sc")
         nc.vector.memset(w3_sc[:].rearrange("p a c -> p (a c)").bitcast(I32), 0)
-        identity = held([P, P], F32, "identity")
-        make_identity(nc, identity[:])
 
         w1_rows = w1.rearrange("(p j) c -> p j c", j=4)
         w2_flat = w2_words[0].rearrange("p c i -> p (c i)").bitcast(I32)

from contextlib import ExitStack

import concourse.mybir as mybir
from concourse.masks import make_identity

K, H, N, T, S = 512, 1024, 768, 4096, 1024
FLOPS = 2 * K * H * S * 2 + 2 * H * N * S

F32 = mybir.dt.float32
BF16 = mybir.dt.bfloat16
I32 = mybir.dt.int32
U32 = mybir.dt.uint32
U16 = mybir.dt.uint16
U8 = mybir.dt.uint8
FP8X4 = mybir.dt.float8_e4m3fn_x4
FP4X4 = mybir.dt.float4_e2m1fn_x4
ACT = mybir.ActivationFunctionType
ALU = mybir.AluOpType

P = 128
KIB = 1024
HALF = 512
QUART = 256
NT = N // P
ROWS_AT = P - 16
SCALAR_SHARE = 160
GPSIMD_SHARE = 256
TURNED = ((0, 3), (1, 2), (1, 3))
FILL_AT = 24 * KIB
SIG_AT = 50 * KIB
TABLE_AT = 58 * KIB
ROWS_BF_AT = 66 * KIB
W1_RAW_AT = 0
W1_BF_AT = 16 * KIB
H_BF_AT = 28 * KIB
LAST_HOURS_AT = 38 * KIB
PROD_AT = 76 * KIB


def tile_list_measles_interchange_tracing_kernel(
    tc, tab_words, tab_scales, offs, offs2, w1, w2_words, w2_scales, bias, gain,
    w3_words, w3_scales, hours, sus, out,
):
    nc = tc.nc
    with ExitStack() as ctx:
        lists = ctx.enter_context(tc.tile_pool(name="lists", bufs=1))
        keep = ctx.enter_context(tc.tile_pool(name="keep", bufs=1))
        shared = ctx.enter_context(tc.tile_pool(name="shared", bufs=1))
        psum = ctx.enter_context(tc.psum_pool(name="psum", bufs=1))

        def bank(i, shape=(P, HALF)):
            return psum.tile(list(shape), F32, name="bank%d" % i, tag="bank%d" % i)

        def held(shape, dtype, name, tag=None):
            return keep.tile(shape, dtype, name=name, tag=tag or name, align_bytes=64)

        def placed(shape, dtype, name, offset):
            return shared.tile(shape, dtype, name=name, offset=offset, align_bytes=64)

        identity = held([P, P], F32, "identity")
        make_identity(nc, identity[:])
        warm = held([P, 8], F32, "warm")
        nc.scalar.activation(warm[:, 0:1], identity[:, 0:1], ACT.Sigmoid)

        list_a = lists.tile([P, S // 16], U16, name="list_a")
        list_b = lists.tile([P, S // 16], U16, name="list_b")
        table_sc = held([P, T], U8, "table_sc")
        nc.sync.dma_start(table_sc[ROWS_AT:P].bitcast(I32), tab_scales[0].bitcast(I32))
        nc.sync.dma_start(list_a[:], offs)
        nc.sync.dma_start(list_b[:], offs2)
        both = (list_a, list_b)

        def load_scale_rows(plane, rows):
            for r in range(4):
                nc.sync.dma_start(plane[r:P:32].bitcast(I32), rows[r:16:4].bitcast(I32))

        table = placed([P, T], U16, "table", TABLE_AT)
        w2_sc_raw = held([P, H], U8, "w2_sc_raw")
        nc.vector.memset(w2_sc_raw[:].bitcast(I32), 0)
        const_rows = held([P, HALF], F32, "const_rows")
        nc.vector.memset(const_rows[:], 0.0)
        nc.vector.memset(table_sc[0:ROWS_AT].bitcast(I32), 0)
        plane_early = held([P, 3 * HALF], U8, "plane_early")
        plane_late = held([P, HALF], U8, "plane_late")
        nc.vector.memset(plane_early[:].bitcast(I32), 0)
        nc.vector.memset(plane_late[:].bitcast(I32), 0)
        nc.sync.dma_start(table[:].bitcast(I32), tab_words[0].bitcast(I32))
        nc.sync.dma_start(const_rows[0:2, :], gain.rearrange("(b c) -> b c", b=2))
        nc.sync.dma_start(const_rows[2:4, :], bias.rearrange("(b c) -> b c", b=2))
        load_scale_rows(w2_sc_raw, w2_scales[0])

        w3_sc = held([P, 2, N], U8, "w3_sc")
        nc.vector.memset(w3_sc[:].rearrange("p a c -> p (a c)").bitcast(I32), 0)

        w1_rows = w1.rearrange("(p j) c -> p j c", j=4)
        w2_flat = w2_words[0].rearrange("p c i -> p (c i)").bitcast(I32)
        w1_raw, w2_raw = [], []

        def load_w1(piece):
            w1_raw.append(placed([P, 4, QUART], F32, "w1_raw%d" % piece, W1_RAW_AT + 16 * QUART * piece))
            nc.sync.dma_start(w1_raw[piece][:], w1_rows[:, :, piece * QUART : (piece + 1) * QUART])

        def load_w2(b):
            w2_raw.append(held([P, HALF], U32, "w2_raw%d" % b))
            nc.sync.dma_start(w2_raw[b][:].bitcast(I32), w2_flat[:, b * HALF : (b + 1) * HALF])

        load_w1(0)
        load_w1(1)
        load_w2(0)

        consts_ps = bank(7, (P, P, 4))
        for t in range(4):
            nc.tensor.transpose(consts_ps[:, :, t], const_rows[:, t:HALF:4], identity[:])
        consts = held([P, 4, 4], F32, "consts")
        nc.scalar.copy(consts[:], consts_ps[:, 0:4, :])

        v_words = {}
        v_sc = {(0, 0): plane_early[:, 0:HALF], (0, 1): plane_early[:, HALF:S], (1, 0): plane_early[:, S : S + HALF],
                (1, 1): plane_late[:]}

        def gather(store, window, k, half, dst):
            cols = slice(half * HALF // 16, (half + 1) * HALF // 16)
            store[k, half] = dst[:]
            nc.vector.tensor_copy(dst[:], window[:].indirect(both[k][:, cols]))

        def carry(plane, picked):
            for r in range(4):
                nc.sync.dma_start(plane[r:P:32].bitcast(I32), picked[ROWS_AT + r : P : 4].bitcast(I32))

        picked_early = held([P, 3 * HALF], U8, "picked_early")
        nc.vector.tensor_copy(picked_early[:, 0:S], table_sc[:].indirect(list_a[:]))
        nc.vector.tensor_copy(picked_early[:, S : S + HALF], table_sc[:].indirect(list_b[:, 0 : HALF // 16]))
        carry(plane_early, picked_early)
        load_w1(2)
        load_w1(3)
        load_w2(1)
        load_scale_rows(w3_sc, w3_scales.rearrange("a r c -> r a c"))
        w3_codes = held([P, 2, 2 * N], U8, "w3_codes")
        nc.sync.dma_start(w3_codes[:].bitcast(I32), w3_words.rearrange("a p c -> p a c").bitcast(I32))
        given = {}

        def load_given(x, n0, n1, halves, tile=None):
            if tile is None:
                tile = held([P, n1 - n0, len(halves) * HALF], F32, "given%d%d%d" % (x, n0, halves[0]))
            rows = (hours, sus)[x].rearrange("(n p) j -> p n j", p=P)
            nc.sync.dma_start(tile[:], rows[:, n0:n1, halves[0] * HALF : (halves[-1] + 1) * HALF])
            for n in range(n0, n1):
                for i, half in enumerate(halves):
                    given[x, half, n] = tile[:, n - n0, i * HALF : (i + 1) * HALF]

        def given_row(x, half, n):
            return given[x, half, n]

        load_given(0, 0, 1, (0, 1))
        for k in range(2):
            gather(v_words, table, k, 0, held([P, HALF], U16, "words0_%d" % k))

        w_codes = {(k, b): held([P, HALF], U32, "w%d_codes%d" % (k, b)) for k in range(2) for b in range(2)}
        w_sc = [held([P, H], U8, "w%d_sc" % k) for k in (1, 2)]

        def deal(dst, src):
            nc.vector.tensor_copy(dst.rearrange("p (b t m) -> p b m t", t=4, m=P),
                                  src.rearrange("p (b m t) -> p b m t", t=4, m=P))

        def prepare_weights(b):
            cols = slice(b * HALF, (b + 1) * HALF)
            w1_bf = placed([P, 4 * HALF], BF16, "w1_bf%d" % b, W1_BF_AT + 8 * HALF * b)
            dealt = w1_bf[:].rearrange("p (t m j) -> p m j t", t=4, j=4)
            for piece in range(2):
                src = w1_raw[2 * b + piece][:].rearrange("p j (m t) -> p m j t", t=4)
                copy = nc.vector.tensor_copy if 2 * b + piece == 3 else nc.scalar.copy
                copy(dealt[:, piece * QUART // 4 : (piece + 1) * QUART // 4], src)
            deal(w_codes[1, b][:], w2_raw[b][:])
            nc.vector.quantize_mx(out=w_codes[0, b][:].bitcast(FP8X4), scales=w_sc[0][:, cols], in_=w1_bf[:])

        deal(w_sc[1][:], w2_sc_raw[:])
        prepare_weights(0)
        picked_late = placed([P, HALF], U8, "picked_late", W1_BF_AT)
        nc.vector.tensor_copy(picked_late[:], table_sc[:].indirect(list_b[:, HALF // 16 : S // 16]))
        carry(plane_late, picked_late)
        load_given(0, 1, 2, (0, 1))
        load_given(0, 2, 4, (0, 1))
        load_given(1, 0, 2, (0,))
        load_given(0, 4, 6, (0, 1), placed([P, 2, S], F32, "last_hours", LAST_HOURS_AT))
        load_given(1, 2, 4, (0,))
        load_given(1, 4, 6, (0,))
        load_given(1, 0, 2, (1,))
        load_given(1, 2, 6, (1,))
        prepare_weights(1)
        for k in range(2):
            gather(v_words, table, k, 1, placed([P, HALF], U16, "words1_%d" % k, W1_BF_AT + (8 + 2 * k) * HALF))

        def first_product(half, b, sig):
            accs = [bank((4 * (2 * half + b) + t) % 7) for t in range(4)]

            def one_pass(t, k, start):
                wc = slice(b * HALF + t * P, b * HALF + (t + 1) * P)
                nc.tensor.matmul_mx(
                    out=accs[t][:], lhsT=w_codes[k, b][:, t * P : (t + 1) * P].bitcast(FP8X4), lhsT_scale=w_sc[k][:, wc],
                    rhs=v_words[k, half].bitcast(FP4X4), rhs_scale=v_sc[k, half], start=start, stop=not start)

            ahead = 2 if half == 0 and b == 0 else 0
            for t in range(ahead):
                one_pass(t, 1, True)
            for t in range(4):
                if t >= ahead:
                    one_pass(t, 1, True)
                one_pass(t, 0, False)
                nc.scalar.activation(sig[:, t, :], accs[t][:], ACT.Sigmoid, bias=consts[:, 2 + b, t : t + 1])
            return sig

        h_bf = {(0, 0): placed([P, 4 * HALF], BF16, "h_bf00", TABLE_AT), (0, 1): held([P, 4 * HALF], BF16, "h_bf01")}
        for b in range(2):
            h_bf[1, b] = placed([P, 4 * HALF], BF16, "h_bf1%d" % b, H_BF_AT + 5 * KIB * b)
        units = [(half, b) for half in range(2) for b in range(2)]
        h_codes = {}
        h_sc = {u: held([P, HALF], U8, "h_sc%d%d" % u) for u in units}
        sig = {}

        def gain_on_vector(half, b, c0, c1):
            nc.vector.tensor_tensor(
                h_bf[half, b][:, 4 * c0 : 4 * c1].rearrange("p (c i t) -> p c t i", i=2, t=4),
                sig[half, b][:, :, c0:c1].rearrange("p t (c i) -> p c t i", i=2),
                consts_ps[:, b, :].unsqueeze(1).unsqueeze(3).to_broadcast([P, (c1 - c0) // 2, 4, 2]), ALU.mult)

        def gain_on_gpsimd(half, b, c0, c1):
            nc.gpsimd.tensor_tensor(
                h_bf[half, b][:, 4 * c0 : 4 * c1].rearrange("p (c t) -> p c t", t=4),
                sig[half, b][:, :, c0:c1].rearrange("p t c -> p c t"),
                consts[:, b, :].unsqueeze(1).to_broadcast([P, c1 - c0, 4]), ALU.mult)

        def gain_on_scalar(half, b, c0, c1):
            h_rows = placed([P, 4, c1 - c0], BF16, "h_rows%d" % b, ROWS_BF_AT + 4 * KIB * b)
            for t in range(4):
                nc.scalar.activation(h_rows[:, t, :], sig[half, b][:, t, c0:c1], ACT.Copy, scale=consts[:, b, t : t + 1])
            nc.scalar.copy(h_bf[half, b][:, 4 * c0 : 4 * c1].rearrange("p (c i t) -> p c t i", i=4, t=4),
                           h_rows[:].rearrange("p t (c i) -> p c t i", i=4))

        def quantise(half, b, codes):
            h_codes[half, b] = codes
            nc.vector.quantize_mx(out=codes[:].bitcast(FP8X4), scales=h_sc[half, b][:], in_=h_bf[half, b][:])

        out_v = out.rearrange("(n p) j -> p n j", p=P)
        accs, prods, turned = {}, {}, {}

        def second_pass(half, n, b, start):
            nc.tensor.matmul_mx(
                out=accs[half, n][:], lhsT=w3_codes[:, b, 2 * P * n : 2 * P * (n + 1)].bitcast(FP4X4),
                lhsT_scale=w3_sc[:, b, P * n : P * (n + 1)],
                rhs=h_codes[half, b][:].bitcast(FP8X4), rhs_scale=h_sc[half, b][:], start=start, stop=not start)

        def open_bank(half, n, i, b=0):
            accs[half, n] = bank(i)
            second_pass(half, n, b, True)

        def weigh(half, n, at=None, b=1):
            second_pass(half, n, b, False)
            name = "prod%d%d" % (half, n)
            prods[half, n] = held([P, HALF], F32, name) if at is None else placed([P, HALF], F32, name, at)
            if (half, n) in TURNED:
                nc.vector.scalar_tensor_tensor(prods[half, n][:], accs[half, n][:], -1.0, given_row(0, half, n),
                                               ALU.mult, ALU.mult)
            else:
                nc.vector.tensor_tensor(prods[half, n][:], given_row(0, half, n), accs[half, n][:], ALU.mult)

        def store(half, n, score):
            nc.sync.dma_start(out_v[:, n, half * HALF : (half + 1) * HALF], score[:])

        def subtract(engine, half, n, at=None, c0=0, c1=HALF):
            name = "score%d%d_%d" % (half, n, c0)
            score = held([P, c1 - c0], F32, name) if at is None else placed([P, c1 - c0], F32, name, at)
            engine.tensor_tensor(score[:], given_row(1, half, n)[:, c0:c1], prods[half, n][:, c0:c1], ALU.subtract)
            nc.sync.dma_start(out_v[:, n, half * HALF + c0 : half * HALF + c1], score[:])

        def turn_and_add(half, n, i):
            total = bank(i)
            for x, rows in enumerate((given_row(1, half, n), prods[half, n])):
                for c in range(0, HALF, P):
                    nc.tensor.matmul(total[:, c : c + P], rows[:, c : c + P], identity[:], is_transpose=True,
                                     start=x == 0 and c == 0, stop=x == 1 and c == HALF - P)
            name = "turned%d%d" % (half, n)
            turned[half, n] = held([P, HALF], F32, name) if half else placed([P, HALF], F32, name, ROWS_BF_AT + 4 * KIB)
            nc.scalar.copy(turned[half, n][:], total[:])

        def turn_back(half, n, i):
            total = bank(i)
            for c in range(0, HALF, P):
                nc.tensor.transpose(total[:, c : c + P], turned[half, n][:, c : c + P], identity[:])
            score = held([P, HALF], F32, "score%d%d" % (half, n))
            nc.scalar.copy(score[:], total[:])
            store(half, n, score)

        sig[0, 0] = first_product(0, 0, placed([P, 4, HALF], F32, "sig00", W1_RAW_AT + 4 * KIB))
        sig[0, 1] = first_product(0, 1, placed([P, 4, HALF], F32, "sig01", SIG_AT))
        gain_on_vector(0, 0, 0, HALF - GPSIMD_SHARE)
        gain_on_gpsimd(0, 0, HALF - GPSIMD_SHARE, HALF)
        sig[1, 0] = first_product(1, 0, held([P, 4, HALF], F32, "sig10"))
        gain_on_vector(0, 1, 0, HALF)
        quantise(0, 0, placed([P, HALF], U32, "h_codes00", SIG_AT))
        quantise(0, 1, held([P, HALF], U32, "h_codes01"))
        gain_on_vector(1, 0, 0, HALF - SCALAR_SHARE)
        gain_on_scalar(1, 0, HALF - SCALAR_SHARE, HALF)
        sig[1, 1] = first_product(1, 1, held([P, 4, HALF], F32, "sig11"))
        gain_on_scalar(1, 1, 0, HALF)
        open_bank(0, 0, 2)
        open_bank(0, 1, 3)
        weigh(0, 0)
        quantise(1, 0, held([P, HALF], U32, "h_codes10"))
        subtract(nc.gpsimd, 0, 0, H_BF_AT)
        weigh(0, 1, PROD_AT)
        subtract(nc.gpsimd, 0, 1)
        for n in range(2, NT):
            open_bank(0, n, (n + 2) % 7)
            weigh(0, n, FILL_AT if n == 4 else None)
        for n, i in enumerate((1, 2, 3, 4)):
            open_bank(1, n, i)
        turn_and_add(0, 3, 7)
        open_bank(1, 4, 6)
        open_bank(1, 5, 0)
        subtract(nc.vector, 0, 2, PROD_AT - 2 * KIB + 64)
        subtract(nc.vector, 0, 4, PROD_AT + 64)
        quantise(1, 1, placed([P, HALF], U32, "h_codes11", FILL_AT))
        subtract(nc.vector, 0, 5, H_BF_AT + 5 * KIB)
        for n in range(NT):
            weigh(1, n)
            if n < 2:
                subtract(nc.gpsimd, 1, n)
            if n == 2:
                turn_back(0, 3, 5)
        turn_and_add(1, 2, 1)
        turn_and_add(1, 3, 2)
        turn_back(1, 2, 7)
        turn_back(1, 3, 5)
        for n in (4, 5):
            subtract(nc.vector, 1, n, LAST_HOURS_AT + 2 * KIB * (n - 4))
